import numpy as np
import ml_dtypes


def mxq(x, axis, fmt="e4m3"):
    dtype, down = {"e4m3": (ml_dtypes.float8_e4m3fn, 7), "e5m2": (ml_dtypes.float8_e5m2, 14)}[fmt]
    v = np.moveaxis(np.asarray(x, np.float32).astype(ml_dtypes.bfloat16).astype(np.float64), axis, -1)
    blocks = v.reshape(v.shape[:-1] + (-1, 32))
    amax = np.abs(blocks).max(-1, keepdims=True)
    byte = np.maximum(np.where(amax > 0, np.frexp(amax)[1] - 1 + 127, 0) - down, 1)
    scale = np.exp2(byte - 127.0)
    codes = (blocks / scale).astype(np.float32).astype(dtype).astype(np.float64)
    return np.moveaxis((codes * scale).reshape(v.shape), -1, axis)


WIDE = False


def mx_kscale(k):
    if not WIDE:
        return np.ones(k)
    levels = np.array([10, -10, 5, -5, 0])
    if k % 512:
        return np.exp2(np.random.permutation(np.resize(levels, k // 32))).repeat(32)
    a = np.empty((k // 512, 16))
    for p in range(k // 512):
        a[p, :8] = np.random.permutation(np.resize(levels, 8))
        for g in range(8):
            far = levels[np.abs(levels - a[p, g]) >= 10]
            a[p, g + 8] = far[np.random.randint(len(far))]
    return np.exp2(a.ravel()).repeat(32)


def f64(x):
    return np.asarray(x).astype(np.float64)


def striped(idx):
    return np.tile(idx.reshape(-1, 16).T, (8, 1)).astype(np.uint16)


def unstriped(offs):
    return offs[:16].T.reshape(-1).astype(np.int64)


E2M1 = np.array([0.0, 0.5, 1.0, 1.5, 2.0, 3.0, 4.0, 6.0, -0.0, -0.5, -1.0, -1.5, -2.0, -3.0, -4.0, -6.0])


def pack_weight(w, fmt):
    k, n = w.shape
    w = f64(np.asarray(w, np.float32).astype(ml_dtypes.bfloat16)).reshape(k // 32, 32, n)
    amax = np.abs(w).max(1)
    if fmt == "e4m3":
        byte = np.frexp(amax)[1] - 1 + 127 - 7
    else:
        mant, ex = np.frexp(amax / 6.0)
        byte = np.where(mant > 0.5, ex, ex - 1) + 127
    byte = np.clip(np.where(amax > 0, byte, 1), 1, 254)
    scaled = (w * np.exp2(127.0 - byte)[:, None, :]).reshape(k, n).astype(np.float32)
    by_word = np.ascontiguousarray(scaled.reshape(k // 512, 128, 4, n).transpose(0, 1, 3, 2))
    if fmt == "e4m3":
        words = by_word.astype(ml_dtypes.float8_e4m3fn).view(np.uint8)
    else:
        c = by_word.astype(ml_dtypes.float4_e2m1fn).view(np.uint8) & 0xF
        words = (c[..., 0::2] | (c[..., 1::2] << 4)).reshape(k // 512, 128, 2 * n)
    return np.ascontiguousarray(words), np.ascontiguousarray(byte.astype(np.uint8).reshape(k // 512, 16, n))


def unpack_weight(words, scales, fmt):
    g, _, n = scales.shape
    words = np.ascontiguousarray(words).reshape(g, 128, n, -1)
    if fmt == "e4m3":
        vals = words.view(ml_dtypes.float8_e4m3fn).astype(np.float64)
    else:
        nib = np.empty((g, 128, n, 4), np.uint8)
        nib[..., 0::2] = words & 0xF
        nib[..., 1::2] = words >> 4
        vals = E2M1[nib]
    vals = vals * np.repeat(np.exp2(scales.astype(np.float64) - 127.0), 8, axis=1)[..., None]
    return vals.transpose(0, 1, 3, 2).reshape(g * 512, n)


def gelu(v):
    return 0.5 * v * (1.0 + np.tanh(np.sqrt(2.0 / np.pi) * (v + 0.044715 * v**3)))


K, H, N, T, S, T2, P = 1536, 512, 768, 2048, 1024, 2048, 128

def setup_inputs():
    n = np.random.standard_normal
    s = mx_kscale(K)[:, None]
    u = mx_kscale(H)[:, None]
    tab_words, tab_scales = pack_weight(n((K, T)) * s, "e4m3")
    wsk_words, wsk_scales = pack_weight(n((K, N)) / np.sqrt(K) / s, "e2m1")
    return {
        "tab_words": tab_words, "tab_scales": tab_scales,
        "offs": striped(np.random.permutation(T)[:S]),
        "wenc": (n((K, H)) / np.sqrt(K) / s * u.T).astype(np.float32),
        "benc": (0.5 * n(H) * u[:, 0]).astype(np.float32),
        "wdec": (1.3 * n((H, N)) / np.sqrt(H) / u).astype(np.float32),
        "wsk_words": wsk_words, "wsk_scales": wsk_scales,
        "wgo": np.exp(0.3 * n((P, S))).astype(np.float32),
        "offs2": striped(np.random.permutation(T2)[:S]),
    }

def reference(tab_words, tab_scales, offs, wenc, benc, wdec, wsk_words, wsk_scales, wgo, offs2):
    v = unpack_weight(tab_words, tab_scales, "e4m3")[:, unstriped(offs)]
    wsk = unpack_weight(wsk_words, wsk_scales, "e2m1")
    we = mxq(f64(wenc), 0, "e4m3")
    wd = mxq(f64(wdec), 0, "e4m3")
    h = np.maximum((we.T @ v) + f64(benc)[:, None], 0.0)
    hq = mxq(h, 0, "e4m3")
    decoded = wd.T @ hq
    original = wsk.T @ v
    y = np.abs(original - decoded)
    out = np.zeros((N, T2))
    out[:, unstriped(offs2)] = np.tile(f64(wgo), (N // P, 1)) * y
    return out

@@ -1,0 +1,236 @@
+from contextlib import ExitStack
+
+import concourse.mybir as mybir
+
+K, H, N, T, S, T2, P = 1536, 512, 768, 2048, 1024, 2048, 128
+FLOPS = 2 * S * (K * H + H * N + K * N)
+
+F32 = mybir.dt.float32
+BF16 = mybir.dt.bfloat16
+I32 = mybir.dt.int32
+U32 = mybir.dt.uint32
+U16 = mybir.dt.uint16
+U8 = mybir.dt.uint8
+FP8X4 = mybir.dt.float8_e4m3fn_x4
+FP4X4 = mybir.dt.float4_e2m1fn_x4
+ACT = mybir.ActivationFunctionType
+ALU = mybir.AluOpType
+
+PASSES = K // 512
+ROW_TILES = N // P
+CHUNKS = ((0, 256), (256, 512), (512, 1024))
+DEC_CHUNKS = ((0, 128), (128, 256), (256, 512), (512, 768))
+CACHE_BUFS = 4
+
+
+def tile_list_shortlist_coding_residual_kernel(
+    tc, tab_words, tab_scales, offs, wenc, benc, wdec, wsk_words, wsk_scales, wgo, offs2, out
+):
+    nc = tc.nc
+    with ExitStack() as ctx:
+        keep = ctx.enter_context(tc.tile_pool(name="keep", bufs=1))
+        ring = ctx.enter_context(tc.tile_pool(name="ring", bufs=3))
+        enc_psum = ctx.enter_context(tc.psum_pool(name="enc_psum", bufs=1))
+        res_psum = ctx.enter_context(tc.psum_pool(name="res_psum", bufs=4))
+
+        pick = keep.tile([P, S // 16], U16, name="pick")
+        place = keep.tile([P, S // 16], U16, name="place")
+        tab_w = [keep.tile([P, T], I32, name="tab_w%d" % a, align_bytes=64) for a in range(PASSES)]
+        tab_s = keep.tile([P, T // 4], I32, name="tab_s", align_bytes=64)
+        doc_w = [keep.tile([P, S], U32, name="doc_w%d" % a, align_bytes=64) for a in range(PASSES)]
+        doc_s_rows = keep.tile([P, S], U8, name="doc_s_rows", align_bytes=64)
+        doc_s = keep.tile([P, 4, S // 4], I32, name="doc_s", align_bytes=64)
+        enc_raw = [keep.tile([P, 4, H], F32, name="enc_raw%d" % a) for a in range(PASSES)]
+        enc_bf = [keep.tile([P, 4, P, 4], BF16, name="enc_bf%d" % a, align_bytes=64) for a in range(PASSES)]
+        enc_w = [keep.tile([P, H], U32, name="enc_w%d" % a, align_bytes=64) for a in range(PASSES)]
+        enc_s = [keep.tile([P, H], U8, name="enc_s%d" % a, align_bytes=64) for a in range(PASSES)]
+        bias = keep.tile([P, 4], F32, name="bias")
+        dec_raw = [keep.tile([P, 4, c1 - c0], F32, name="dec_raw%d" % c0) for c0, c1 in DEC_CHUNKS]
+        dec_bf = keep.tile([P, N, 4], BF16, name="dec_bf", align_bytes=64)
+        dec_w = keep.tile([P, N], U32, name="dec_w", align_bytes=64)
+        dec_s = keep.tile([P, N], U8, name="dec_s", align_bytes=64)
+        sk_w = keep.tile([P, PASSES, 2 * N // 4], I32, name="sk_w", align_bytes=64)
+        sk_s = keep.tile([P, PASSES, N // 4], I32, name="sk_s", align_bytes=64)
+        weight = keep.tile([P, S], F32, name="weight")
+        code_bf = keep.tile([P, S, 4], BF16, name="code_bf", align_bytes=64)
+        code_w = keep.tile([P, S], U32, name="code_w", align_bytes=64)
+        code_s = keep.tile([P, S], U8, name="code_s", align_bytes=64)
+        cache = [keep.tile([P, T2], F32, name="cache%d" % b) for b in range(CACHE_BUFS)]
+
+        nc.vector.memset(tab_s[:], 0)
+        nc.vector.memset(sk_s[:], 0)
+        nc.vector.memset(doc_s[:], 0)
+        nc.sync.dma_start(pick[:], offs)
+        for a in range(PASSES):
+            nc.scalar.dma_start(tab_s[a:64:4, :], tab_scales[a].bitcast(I32))
+        nc.scalar.dma_start(bias[:], benc.rearrange("(p t) -> p t", t=4))
+        for q in range(4):
+            nc.scalar.dma_start(
+                sk_s[32 * q : 32 * q + 4, :, :],
+                wsk_scales[:, 4 * q : 4 * q + 4, :].bitcast(I32).rearrange("a r n -> r a n"),
+            )
+        for a in range(PASSES):
+            nc.sync.dma_start(tab_w[a][:], tab_words[a].rearrange("p t i -> p (t i)").bitcast(I32))
+            rows = wenc[512 * a : 512 * (a + 1), :].rearrange("(p j) c -> p j c", j=4)
+            if a < PASSES - 1:
+                nc.sync.dma_start(enc_raw[a][:], rows)
+            else:
+                nc.sync.dma_start(enc_raw[a][:, :, 0:256], rows[:, :, 0:256])
+                nc.sync.dma_start(enc_raw[a][:, :, 256:512], rows[:, :, 256:512])
+        dec_rows = wdec.rearrange("(p j) n -> p j n", j=4)
+        nc.sync.dma_start(dec_raw[0][:], dec_rows[:, :, 0:128])
+        nc.sync.dma_start(sk_w[:], wsk_words.bitcast(I32).rearrange("a p c -> p a c"))
+        nc.sync.dma_start(place[:], offs2)
+        nc.sync.dma_start(weight[:, 0:256], wgo[:, 0:256])
+        for d in range(1, len(DEC_CHUNKS)):
+            c0, c1 = DEC_CHUNKS[d]
+            nc.sync.dma_start(dec_raw[d][:], dec_rows[:, :, c0:c1])
+        nc.sync.dma_start(weight[:, 256:S], wgo[:, 256:S])
+
+        for b in range(2):
+            nc.vector.memset(cache[b][:], 0.0)
+
+        nc.vector.tensor_copy(doc_s_rows[:], tab_s[:].bitcast(U8).indirect(pick[:]))
+        for q in range(4):
+            nc.scalar.dma_start(doc_s[32 * q : 32 * q + 4, :, :], doc_s_rows[16 * q : 16 * q + 16, :].bitcast(I32))
+
+        def gather_words(a, j0, j1):
+            nc.vector.tensor_copy(doc_w[a][:, j0:j1], tab_w[a][:].bitcast(U32).indirect(pick[:, j0 // 16 : j1 // 16]))
+
+        def cast_enc(engine_copy, a, m0, m1):
+            engine_copy(
+                enc_bf[a][:, :, m0:m1, :].rearrange("p t m j -> p m j t"),
+                enc_raw[a][:, :, 4 * m0 : 4 * m1].rearrange("p j (m t) -> p m j t", t=4),
+            )
+
+        def quant_enc(a, t0, t1):
+            nc.vector.quantize_mx(
+                out=enc_w[a][:, t0 * P : t1 * P].bitcast(FP8X4),
+                scales=enc_s[a][:, t0 * P : t1 * P],
+                in_=enc_bf[a][:, t0:t1, :, :].rearrange("p t m j -> p (t m j)"),
+            )
+
+        def cast_dec(d):
+            c0, c1 = DEC_CHUNKS[d]
+            nc.scalar.activation(
+                dec_bf[:, c0:c1, :].rearrange("p (c i) j -> p c j i", i=4),
+                dec_raw[d][:].rearrange("p j (c i) -> p c j i", i=4),
+                ACT.Copy,
+                scale=-1.0,
+            )
+
+        def quant_dec(d):
+            c0, c1 = DEC_CHUNKS[d]
+            nc.vector.quantize_mx(
+                out=dec_w[:, c0:c1].bitcast(FP8X4),
+                scales=dec_s[:, c0:c1],
+                in_=dec_bf[:, c0:c1, :].rearrange("p c j -> p (c j)"),
+            )
+
+        def doc_operand(a, j0, j1):
+            return doc_w[a][:, j0:j1].bitcast(FP8X4), doc_s[:, a, :].bitcast(U8)[:, j0:j1]
+
+        def encode(j0, j1, interleave):
+            width = j1 - j0
+            banks = [enc_psum.tile([P, 512], F32, name="enc_bank%d" % t) for t in range(4)]
+            for a in range(PASSES):
+                rhs, rhs_scale = doc_operand(a, j0, j1)
+                for t in range(4):
+                    nc.tensor.matmul_mx(
+                        out=banks[t][:, 0:width],
+                        lhsT=enc_w[a][:, t * P : (t + 1) * P].bitcast(FP8X4),
+                        lhsT_scale=enc_s[a][:, t * P : (t + 1) * P],
+                        rhs=rhs,
+                        rhs_scale=rhs_scale,
+                        start=(a == 0),
+                        stop=(a == PASSES - 1),
+                    )
+            planes = ring.tile([P, 4, 512], BF16, name="planes")
+            for t in range(4):
+                nc.scalar.activation(planes[:, t, 0:width], banks[t][:, 0:width], ACT.Relu, bias=bias[:, t : t + 1])
+            interleave(
+                code_bf[:, j0:j1, :].rearrange("p (c i) t -> p c t i", i=4),
+                planes[:, :, 0:width].rearrange("p t (c i) -> p c t i", i=4),
+            )
+            nc.vector.quantize_mx(
+                out=code_w[:, j0:j1].bitcast(FP8X4),
+                scales=code_s[:, j0:j1],
+                in_=code_bf[:, j0:j1, :].rearrange("p c t -> p (c t)"),
+            )
+
+        def residual(n, j0, j1, dst):
+            width = j1 - j0
+            step = 512 if width == 512 else 128
+            bank = res_psum.tile([P, 512], F32, name="res_bank")
+            for g0 in range(j0, j1, step):
+                acc = bank[:, g0 - j0 : g0 - j0 + step]
+                for a in range(PASSES):
+                    rhs, rhs_scale = doc_operand(a, g0, g0 + step)
+                    nc.tensor.matmul_mx(
+                        out=acc,
+                        lhsT=sk_w[:, a, :].bitcast(U8)[:, 2 * n * P : 2 * (n + 1) * P].bitcast(FP4X4),
+                        lhsT_scale=sk_s[:, a, :].bitcast(U8)[:, n * P : (n + 1) * P],
+                        rhs=rhs,
+                        rhs_scale=rhs_scale,
+                        start=(a == 0),
+                        stop=False,
+                    )
+                nc.tensor.matmul_mx(
+                    out=acc,
+                    lhsT=dec_w[:, n * P : (n + 1) * P].bitcast(FP8X4),
+                    lhsT_scale=dec_s[:, n * P : (n + 1) * P],
+                    rhs=code_w[:, g0 : g0 + step].bitcast(FP8X4),
+                    rhs_scale=code_s[:, g0 : g0 + step],
+                    start=False,
+                    stop=True,
+                )
+            nc.scalar.activation(dst, bank[:, 0:width], ACT.Abs)
+
+        def scatter(n, j0, j1):
+            size = ring.tile([P, S], F32, name="size")
+            for g0 in range(j0, j1, 512):
+                g1 = min(g0 + 512, j1)
+                residual(n, g0, g1, size[:, g0 - j0 : g1 - j0])
+            window = cache[n % CACHE_BUFS]
+            nc.vector.tensor_tensor(
+                window[:].indirect(place[:, j0 // 16 : j1 // 16]), size[:, 0 : j1 - j0], weight[:, j0:j1], ALU.mult
+            )
+            if j1 == S:
+                nc.sync.dma_start(out[n * P : (n + 1) * P, :], window[:])
+
+        for a in range(PASSES - 1):
+            gather_words(a, 0, S)
+            cast_enc(nc.scalar.copy, a, 0, P)
+            quant_enc(a, 0, 4)
+        last = PASSES - 1
+        gather_words(last, 0, 256)
+        gather_words(last, 256, S)
+        cast_enc(nc.scalar.copy, last, 0, 64)
+        cast_enc(nc.vector.tensor_copy, last, 64, P)
+        for t in range(4):
+            quant_enc(last, t, t + 1)
+        cast_dec(0)
+        quant_dec(0)
+
+        encode(0, 256, nc.vector.tensor_copy)
+        scatter(0, 0, 256)
+        cast_dec(1)
+        quant_dec(1)
+        scatter(1, 0, 256)
+        cast_dec(2)
+        quant_dec(2)
+        encode(256, 512, nc.scalar.copy)
+        for b in range(2, CACHE_BUFS):
+            nc.vector.memset(cache[b][:], 0.0)
+        scatter(2, 0, 256)
+        scatter(3, 0, 256)
+        scatter(0, 256, 512)
+        encode(512, 1024, nc.scalar.copy)
+        for n in range(1, CACHE_BUFS):
+            scatter(n, 256, 512)
+        cast_dec(3)
+        quant_dec(3)
+        for n in range(CACHE_BUFS):
+            scatter(n, 512, 1024)
+        for n in range(CACHE_BUFS, ROW_TILES):
+            scatter(n, 0, 1024)

@@ -19,7 +19,7 @@ ALU = mybir.AluOpType
 PASSES = K // 512
 ROW_TILES = N // P
 CHUNKS = ((0, 256), (256, 512), (512, 1024))
-DEC_CHUNKS = ((0, 128), (128, 256), (256, 512), (512, 768))
+DEC_CHUNKS = ((0, 256), (256, 512), (512, 768))
 CACHE_BUFS = 4
 
 
@@ -29,70 +29,79 @@ def tile_list_shortlist_coding_residual_kernel(
     nc = tc.nc
     with ExitStack() as ctx:
         keep = ctx.enter_context(tc.tile_pool(name="keep", bufs=1))
+        stage = ctx.enter_context(tc.tile_pool(name="stage", bufs=5))
         ring = ctx.enter_context(tc.tile_pool(name="ring", bufs=3))
         enc_psum = ctx.enter_context(tc.psum_pool(name="enc_psum", bufs=1))
         res_psum = ctx.enter_context(tc.psum_pool(name="res_psum", bufs=4))
 
         pick = keep.tile([P, S // 16], U16, name="pick")
         place = keep.tile([P, S // 16], U16, name="place")
-        tab_w = [keep.tile([P, T], I32, name="tab_w%d" % a, align_bytes=64) for a in range(PASSES)]
         tab_s = keep.tile([P, T // 4], I32, name="tab_s", align_bytes=64)
         doc_w = [keep.tile([P, S], U32, name="doc_w%d" % a, align_bytes=64) for a in range(PASSES)]
         doc_s_rows = keep.tile([P, S], U8, name="doc_s_rows", align_bytes=64)
         doc_s = keep.tile([P, 4, S // 4], I32, name="doc_s", align_bytes=64)
-        enc_raw = [keep.tile([P, 4, H], F32, name="enc_raw%d" % a) for a in range(PASSES)]
         enc_bf = [keep.tile([P, 4, P, 4], BF16, name="enc_bf%d" % a, align_bytes=64) for a in range(PASSES)]
         enc_w = [keep.tile([P, H], U32, name="enc_w%d" % a, align_bytes=64) for a in range(PASSES)]
         enc_s = [keep.tile([P, H], U8, name="enc_s%d" % a, align_bytes=64) for a in range(PASSES)]
         bias = keep.tile([P, 4], F32, name="bias")
-        dec_raw = [keep.tile([P, 4, c1 - c0], F32, name="dec_raw%d" % c0) for c0, c1 in DEC_CHUNKS]
         dec_bf = keep.tile([P, N, 4], BF16, name="dec_bf", align_bytes=64)
         dec_w = keep.tile([P, N], U32, name="dec_w", align_bytes=64)
         dec_s = keep.tile([P, N], U8, name="dec_s", align_bytes=64)
-        sk_w = keep.tile([P, PASSES, 2 * N // 4], I32, name="sk_w", align_bytes=64)
         sk_s = keep.tile([P, PASSES, N // 4], I32, name="sk_s", align_bytes=64)
-        weight = keep.tile([P, S], F32, name="weight")
         code_bf = keep.tile([P, S, 4], BF16, name="code_bf", align_bytes=64)
         code_w = keep.tile([P, S], U32, name="code_w", align_bytes=64)
         code_s = keep.tile([P, S], U8, name="code_s", align_bytes=64)
         cache = [keep.tile([P, T2], F32, name="cache%d" % b) for b in range(CACHE_BUFS)]
 
-        nc.vector.memset(tab_s[:], 0)
-        nc.vector.memset(sk_s[:], 0)
-        nc.vector.memset(doc_s[:], 0)
-        nc.sync.dma_start(pick[:], offs)
-        for a in range(PASSES):
-            nc.scalar.dma_start(tab_s[a:64:4, :], tab_scales[a].bitcast(I32))
-        nc.scalar.dma_start(bias[:], benc.rearrange("(p t) -> p t", t=4))
-        for q in range(4):
-            nc.scalar.dma_start(
-                sk_s[32 * q : 32 * q + 4, :, :],
-                wsk_scales[:, 4 * q : 4 * q + 4, :].bitcast(I32).rearrange("a r n -> r a n"),
-            )
-        for a in range(PASSES):
+        def staged(shape, dtype, name):
+            return stage.tile(shape, dtype, name=name, tag="staged", align_bytes=64)
+
+        tab_w, enc_raw, dec_raw = [], [], []
+
+        def load_table(a):
+            tab_w.append(staged([P, T], I32, "tab_w%d" % a))
             nc.sync.dma_start(tab_w[a][:], tab_words[a].rearrange("p t i -> p (t i)").bitcast(I32))
+
+        def load_enc(a):
+            enc_raw.append(staged([P, 4, H], F32, "enc_raw%d" % a))
             rows = wenc[512 * a : 512 * (a + 1), :].rearrange("(p j) c -> p j c", j=4)
             if a < PASSES - 1:
                 nc.sync.dma_start(enc_raw[a][:], rows)
             else:
                 nc.sync.dma_start(enc_raw[a][:, :, 0:256], rows[:, :, 0:256])
                 nc.sync.dma_start(enc_raw[a][:, :, 256:512], rows[:, :, 256:512])
-        dec_rows = wdec.rearrange("(p j) n -> p j n", j=4)
-        nc.sync.dma_start(dec_raw[0][:], dec_rows[:, :, 0:128])
-        nc.sync.dma_start(sk_w[:], wsk_words.bitcast(I32).rearrange("a p c -> p a c"))
-        nc.sync.dma_start(place[:], offs2)
-        nc.sync.dma_start(weight[:, 0:256], wgo[:, 0:256])
-        for d in range(1, len(DEC_CHUNKS)):
-            c0, c1 = DEC_CHUNKS[d]
-            nc.sync.dma_start(dec_raw[d][:], dec_rows[:, :, c0:c1])
-        nc.sync.dma_start(weight[:, 256:S], wgo[:, 256:S])
 
-        for b in range(2):
-            nc.vector.memset(cache[b][:], 0.0)
+        def load_dec(d):
+            c0, c1 = DEC_CHUNKS[d]
+            dec_raw.append(staged([P, 4, c1 - c0], F32, "dec_raw%d" % d))
+            nc.sync.dma_start(dec_raw[d][:], wdec.rearrange("(p j) n -> p j n", j=4)[:, :, c0:c1])
+
+        nc.sync.dma_start(pick[:], offs)
+        load_table(0)
+        for a in range(4):
+            nc.sync.dma_start(tab_s[a:64:4, :], tab_scales[a % PASSES].bitcast(I32))
+        nc.gpsimd.memset(tab_s[64:128, :], 0)
+        nc.gpsimd.memset(doc_s[:], 0)
+        nc.gpsimd.memset(sk_s[:], 0)
+        nc.vector.memset(cache[0][:], 0.0)
+        nc.vector.memset(cache[1][:], 0.0)
+        load_enc(0)
+        load_enc(1)
+        load_table(1)
+        load_enc(2)
+        nc.sync.dma_start(place[:], offs2)
+        nc.gpsimd.dma_start(bias[:], benc.rearrange("(p t) -> p t", t=4))
+        for q in range(4):
+            nc.gpsimd.dma_start(
+                sk_s[32 * q : 32 * q + 4, :, :],
+                wsk_scales[:, 4 * q : 4 * q + 4, :].bitcast(I32).rearrange("a r n -> r a n"),
+            )
+        nc.gpsimd.memset(cache[2][:], 0.0)
+        nc.gpsimd.memset(cache[3][:], 0.0)
 
         nc.vector.tensor_copy(doc_s_rows[:], tab_s[:].bitcast(U8).indirect(pick[:]))
         for q in range(4):
-            nc.scalar.dma_start(doc_s[32 * q : 32 * q + 4, :, :], doc_s_rows[16 * q : 16 * q + 16, :].bitcast(I32))
+            nc.sync.dma_start(doc_s[32 * q : 32 * q + 4, :, :], doc_s_rows[16 * q : 16 * q + 16, :].bitcast(I32))
 
         def gather_words(a, j0, j1):
             nc.vector.tensor_copy(doc_w[a][:, j0:j1], tab_w[a][:].bitcast(U32).indirect(pick[:, j0 // 16 : j1 // 16]))
@@ -110,17 +119,16 @@ def tile_list_shortlist_coding_residual_kernel(
                 in_=enc_bf[a][:, t0:t1, :, :].rearrange("p t m j -> p (t m j)"),
             )
 
-        def cast_dec(d):
-            c0, c1 = DEC_CHUNKS[d]
-            nc.scalar.activation(
-                dec_bf[:, c0:c1, :].rearrange("p (c i) j -> p c j i", i=4),
-                dec_raw[d][:].rearrange("p j (c i) -> p c j i", i=4),
-                ACT.Copy,
-                scale=-1.0,
-            )
+        def cast_dec(c0, c1, on_vector):
+            d = c0 // 256
+            dst = dec_bf[:, c0:c1, :].rearrange("p (c i) j -> p c j i", i=4)
+            src = dec_raw[d][:, :, c0 - 256 * d : c1 - 256 * d].rearrange("p j (c i) -> p c j i", i=4)
+            if on_vector:
+                nc.vector.tensor_scalar(dst, src, -1.0, None, ALU.mult)
+            else:
+                nc.scalar.activation(dst, src, ACT.Copy, scale=-1.0)
 
-        def quant_dec(d):
-            c0, c1 = DEC_CHUNKS[d]
+        def quant_dec(c0, c1):
             nc.vector.quantize_mx(
                 out=dec_w[:, c0:c1].bitcast(FP8X4),
                 scales=dec_s[:, c0:c1],
@@ -186,10 +194,10 @@ def tile_list_shortlist_coding_residual_kernel(
                 )
             nc.scalar.activation(dst, bank[:, 0:width], ACT.Abs)
 
-        def scatter(n, j0, j1):
+        def scatter(n, j0, j1, span=512):
             size = ring.tile([P, S], F32, name="size")
-            for g0 in range(j0, j1, 512):
-                g1 = min(g0 + 512, j1)
+            for g0 in range(j0, j1, span):
+                g1 = min(g0 + span, j1)
                 residual(n, g0, g1, size[:, g0 - j0 : g1 - j0])
             window = cache[n % CACHE_BUFS]
             nc.vector.tensor_tensor(
@@ -198,38 +206,46 @@ def tile_list_shortlist_coding_residual_kernel(
             if j1 == S:
                 nc.sync.dma_start(out[n * P : (n + 1) * P, :], window[:])
 
-        for a in range(PASSES - 1):
-            gather_words(a, 0, S)
-            cast_enc(nc.scalar.copy, a, 0, P)
-            quant_enc(a, 0, 4)
         last = PASSES - 1
-        gather_words(last, 0, 256)
-        gather_words(last, 256, S)
+        gather_words(0, 0, S)
+        load_table(last)
+        cast_enc(nc.scalar.copy, 0, 0, P)
+        load_dec(0)
+        cast_enc(nc.scalar.copy, 1, 0, P)
+        sk_w = staged([P, PASSES, 2 * N // 4], I32, "sk_w")
+        nc.sync.dma_start(sk_w[:], wsk_words.bitcast(I32).rearrange("a p c -> p a c"))
+        quant_enc(0, 0, 4)
+        gather_words(1, 0, S)
+        weight = staged([P, S], F32, "weight")
+        nc.sync.dma_start(weight[:, 0:256], wgo[:, 0:256])
+        quant_enc(1, 0, 4)
         cast_enc(nc.scalar.copy, last, 0, 64)
         cast_enc(nc.vector.tensor_copy, last, 64, P)
-        for t in range(4):
-            quant_enc(last, t, t + 1)
-        cast_dec(0)
-        quant_dec(0)
+        load_dec(1)
+        nc.sync.dma_start(weight[:, 256:S], wgo[:, 256:S])
+        quant_enc(last, 0, 4)
+        gather_words(last, 0, 256)
+        gather_words(last, 256, S)
+        load_dec(2)
+        cast_dec(0, 128, True)
+        quant_dec(0, 128)
 
         encode(0, 256, nc.vector.tensor_copy)
-        scatter(0, 0, 256)
-        cast_dec(1)
-        quant_dec(1)
+        scatter(0, 0, 256, 128)
+        cast_dec(128, 256, False)
+        quant_dec(128, 256)
         scatter(1, 0, 256)
-        cast_dec(2)
-        quant_dec(2)
+        cast_dec(256, 512, False)
+        quant_dec(256, 512)
         encode(256, 512, nc.scalar.copy)
-        for b in range(2, CACHE_BUFS):
-            nc.vector.memset(cache[b][:], 0.0)
         scatter(2, 0, 256)
         scatter(3, 0, 256)
         scatter(0, 256, 512)
         encode(512, 1024, nc.scalar.copy)
         for n in range(1, CACHE_BUFS):
             scatter(n, 256, 512)
-        cast_dec(3)
-        quant_dec(3)
+        cast_dec(512, 768, False)
+        quant_dec(512, 768)
         for n in range(CACHE_BUFS):
             scatter(n, 512, 1024)
         for n in range(CACHE_BUFS, ROW_TILES):

@@ -18,9 +18,8 @@ ALU = mybir.AluOpType
 
 PASSES = K // 512
 ROW_TILES = N // P
-CHUNKS = ((0, 256), (256, 512), (512, 1024))
-DEC_CHUNKS = ((0, 256), (256, 512), (512, 768))
-CACHE_BUFS = 4
+STAGED_BUFS = 4
+CACHE_BUFS = 2
 
 
 def tile_list_shortlist_coding_residual_kernel(
@@ -29,17 +28,15 @@ def tile_list_shortlist_coding_residual_kernel(
     nc = tc.nc
     with ExitStack() as ctx:
         keep = ctx.enter_context(tc.tile_pool(name="keep", bufs=1))
-        stage = ctx.enter_context(tc.tile_pool(name="stage", bufs=5))
-        ring = ctx.enter_context(tc.tile_pool(name="ring", bufs=3))
-        enc_psum = ctx.enter_context(tc.psum_pool(name="enc_psum", bufs=1))
-        res_psum = ctx.enter_context(tc.psum_pool(name="res_psum", bufs=4))
+        stage = ctx.enter_context(tc.tile_pool(name="stage", bufs=STAGED_BUFS))
+        psum = ctx.enter_context(tc.psum_pool(name="psum", bufs=1))
 
         pick = keep.tile([P, S // 16], U16, name="pick")
         place = keep.tile([P, S // 16], U16, name="place")
         tab_s = keep.tile([P, T // 4], I32, name="tab_s", align_bytes=64)
         doc_w = [keep.tile([P, S], U32, name="doc_w%d" % a, align_bytes=64) for a in range(PASSES)]
         doc_s_rows = keep.tile([P, S], U8, name="doc_s_rows", align_bytes=64)
-        doc_s = keep.tile([P, 4, S // 4], I32, name="doc_s", align_bytes=64)
+        doc_s = keep.tile([P, PASSES, S // 4], I32, name="doc_s", align_bytes=64)
         enc_bf = [keep.tile([P, 4, P, 4], BF16, name="enc_bf%d" % a, align_bytes=64) for a in range(PASSES)]
         enc_w = [keep.tile([P, H], U32, name="enc_w%d" % a, align_bytes=64) for a in range(PASSES)]
         enc_s = [keep.tile([P, H], U8, name="enc_s%d" % a, align_bytes=64) for a in range(PASSES)]
@@ -51,57 +48,28 @@ def tile_list_shortlist_coding_residual_kernel(
         code_bf = keep.tile([P, S, 4], BF16, name="code_bf", align_bytes=64)
         code_w = keep.tile([P, S], U32, name="code_w", align_bytes=64)
         code_s = keep.tile([P, S], U8, name="code_s", align_bytes=64)
+        planes, size = {}, {}
         cache = [keep.tile([P, T2], F32, name="cache%d" % b) for b in range(CACHE_BUFS)]
 
         def staged(shape, dtype, name):
             return stage.tile(shape, dtype, name=name, tag="staged", align_bytes=64)
 
-        tab_w, enc_raw, dec_raw = [], [], []
+        def bank(b):
+            return psum.tile([P, 512], F32, name="bank%d" % b, tag="bank%d" % b)
+
+        tab_w, enc_raw, dec_raw = {}, {}, {}
 
         def load_table(a):
-            tab_w.append(staged([P, T], I32, "tab_w%d" % a))
+            tab_w[a] = staged([P, T], I32, "tab_w%d" % a)
             nc.sync.dma_start(tab_w[a][:], tab_words[a].rearrange("p t i -> p (t i)").bitcast(I32))
 
         def load_enc(a):
-            enc_raw.append(staged([P, 4, H], F32, "enc_raw%d" % a))
-            rows = wenc[512 * a : 512 * (a + 1), :].rearrange("(p j) c -> p j c", j=4)
-            if a < PASSES - 1:
-                nc.sync.dma_start(enc_raw[a][:], rows)
-            else:
-                nc.sync.dma_start(enc_raw[a][:, :, 0:256], rows[:, :, 0:256])
-                nc.sync.dma_start(enc_raw[a][:, :, 256:512], rows[:, :, 256:512])
+            enc_raw[a] = staged([P, 4, H], F32, "enc_raw%d" % a)
+            nc.sync.dma_start(enc_raw[a][:], wenc[512 * a : 512 * (a + 1), :].rearrange("(p j) c -> p j c", j=4))
 
-        def load_dec(d):
-            c0, c1 = DEC_CHUNKS[d]
-            dec_raw.append(staged([P, 4, c1 - c0], F32, "dec_raw%d" % d))
-            nc.sync.dma_start(dec_raw[d][:], wdec.rearrange("(p j) n -> p j n", j=4)[:, :, c0:c1])
-
-        nc.sync.dma_start(pick[:], offs)
-        load_table(0)
-        for a in range(4):
-            nc.sync.dma_start(tab_s[a:64:4, :], tab_scales[a % PASSES].bitcast(I32))
-        nc.gpsimd.memset(tab_s[64:128, :], 0)
-        nc.gpsimd.memset(doc_s[:], 0)
-        nc.gpsimd.memset(sk_s[:], 0)
-        nc.vector.memset(cache[0][:], 0.0)
-        nc.vector.memset(cache[1][:], 0.0)
-        load_enc(0)
-        load_enc(1)
-        load_table(1)
-        load_enc(2)
-        nc.sync.dma_start(place[:], offs2)
-        nc.gpsimd.dma_start(bias[:], benc.rearrange("(p t) -> p t", t=4))
-        for q in range(4):
-            nc.gpsimd.dma_start(
-                sk_s[32 * q : 32 * q + 4, :, :],
-                wsk_scales[:, 4 * q : 4 * q + 4, :].bitcast(I32).rearrange("a r n -> r a n"),
-            )
-        nc.gpsimd.memset(cache[2][:], 0.0)
-        nc.gpsimd.memset(cache[3][:], 0.0)
-
-        nc.vector.tensor_copy(doc_s_rows[:], tab_s[:].bitcast(U8).indirect(pick[:]))
-        for q in range(4):
-            nc.sync.dma_start(doc_s[32 * q : 32 * q + 4, :, :], doc_s_rows[16 * q : 16 * q + 16, :].bitcast(I32))
+        def load_dec(c0, c1):
+            dec_raw[c0] = staged([P, 4, c1 - c0], F32, "dec_raw%d" % c0)
+            nc.sync.dma_start(dec_raw[c0][:], wdec.rearrange("(p j) n -> p j n", j=4)[:, :, c0:c1])
 
         def gather_words(a, j0, j1):
             nc.vector.tensor_copy(doc_w[a][:, j0:j1], tab_w[a][:].bitcast(U32).indirect(pick[:, j0 // 16 : j1 // 16]))
@@ -112,21 +80,20 @@ def tile_list_shortlist_coding_residual_kernel(
                 enc_raw[a][:, :, 4 * m0 : 4 * m1].rearrange("p j (m t) -> p m j t", t=4),
             )
 
-        def quant_enc(a, t0, t1):
+        def quant_enc(a):
             nc.vector.quantize_mx(
-                out=enc_w[a][:, t0 * P : t1 * P].bitcast(FP8X4),
-                scales=enc_s[a][:, t0 * P : t1 * P],
-                in_=enc_bf[a][:, t0:t1, :, :].rearrange("p t m j -> p (t m j)"),
+                out=enc_w[a][:].bitcast(FP8X4),
+                scales=enc_s[a][:],
+                in_=enc_bf[a][:].rearrange("p t m j -> p (t m j)"),
             )
 
-        def cast_dec(c0, c1, on_vector):
-            d = c0 // 256
-            dst = dec_bf[:, c0:c1, :].rearrange("p (c i) j -> p c j i", i=4)
-            src = dec_raw[d][:, :, c0 - 256 * d : c1 - 256 * d].rearrange("p j (c i) -> p c j i", i=4)
-            if on_vector:
-                nc.vector.tensor_scalar(dst, src, -1.0, None, ALU.mult)
-            else:
-                nc.scalar.activation(dst, src, ACT.Copy, scale=-1.0)
+        def cast_dec(d, c0, c1):
+            nc.scalar.activation(
+                dec_bf[:, c0:c1, :].rearrange("p (c i) j -> p c j i", i=4),
+                dec_raw[d][:, :, c0 - d : c1 - d].rearrange("p j (c i) -> p c j i", i=4),
+                ACT.Copy,
+                scale=-1.0,
+            )
 
         def quant_dec(c0, c1):
             nc.vector.quantize_mx(
@@ -138,115 +105,194 @@ def tile_list_shortlist_coding_residual_kernel(
         def doc_operand(a, j0, j1):
             return doc_w[a][:, j0:j1].bitcast(FP8X4), doc_s[:, a, :].bitcast(U8)[:, j0:j1]
 
-        def encode(j0, j1, interleave):
+        def encode_pass(acc, ts, a, j0, j1):
             width = j1 - j0
-            banks = [enc_psum.tile([P, 512], F32, name="enc_bank%d" % t) for t in range(4)]
-            for a in range(PASSES):
-                rhs, rhs_scale = doc_operand(a, j0, j1)
-                for t in range(4):
-                    nc.tensor.matmul_mx(
-                        out=banks[t][:, 0:width],
-                        lhsT=enc_w[a][:, t * P : (t + 1) * P].bitcast(FP8X4),
-                        lhsT_scale=enc_s[a][:, t * P : (t + 1) * P],
-                        rhs=rhs,
-                        rhs_scale=rhs_scale,
-                        start=(a == 0),
-                        stop=(a == PASSES - 1),
+            rhs, rhs_scale = doc_operand(a, j0, j1)
+            for u, t in enumerate(ts):
+                nc.tensor.matmul_mx(
+                    out=acc[:, u * width : (u + 1) * width],
+                    lhsT=enc_w[a][:, t * P : (t + 1) * P].bitcast(FP8X4),
+                    lhsT_scale=enc_s[a][:, t * P : (t + 1) * P],
+                    rhs=rhs,
+                    rhs_scale=rhs_scale,
+                    start=(a == 0 and u == 0),
+                    stop=(a == PASSES - 1 and u == len(ts) - 1),
+                )
+
+        def relu(acc, ts, j0, j1):
+            width = j1 - j0
+            for g0 in range(j0, j1, 256):
+                if g0 not in planes:
+                    planes[g0] = keep.tile([P, 4, 256], BF16, name="planes%d" % g0, tag="planes%d" % g0, align_bytes=64)
+                for u, t in enumerate(ts):
+                    c0 = u * width + g0 - j0
+                    nc.scalar.activation(
+                        planes[g0][:, t, :], acc[:, c0 : c0 + 256], ACT.Relu, bias=bias[:, t : t + 1]
                     )
-            planes = ring.tile([P, 4, 512], BF16, name="planes")
-            for t in range(4):
-                nc.scalar.activation(planes[:, t, 0:width], banks[t][:, 0:width], ACT.Relu, bias=bias[:, t : t + 1])
-            interleave(
+
+        def interleave(engine_copy, j0, j1):
+            engine_copy(
                 code_bf[:, j0:j1, :].rearrange("p (c i) t -> p c t i", i=4),
-                planes[:, :, 0:width].rearrange("p t (c i) -> p c t i", i=4),
+                planes[j0][:].rearrange("p t (c i) -> p c t i", i=4),
             )
+
+        def quant_code(j0, j1):
             nc.vector.quantize_mx(
                 out=code_w[:, j0:j1].bitcast(FP8X4),
                 scales=code_s[:, j0:j1],
                 in_=code_bf[:, j0:j1, :].rearrange("p c t -> p (c t)"),
             )
 
-        def residual(n, j0, j1, dst):
-            width = j1 - j0
-            step = 512 if width == 512 else 128
-            bank = res_psum.tile([P, 512], F32, name="res_bank")
-            for g0 in range(j0, j1, step):
-                acc = bank[:, g0 - j0 : g0 - j0 + step]
-                for a in range(PASSES):
-                    rhs, rhs_scale = doc_operand(a, g0, g0 + step)
-                    nc.tensor.matmul_mx(
-                        out=acc,
-                        lhsT=sk_w[:, a, :].bitcast(U8)[:, 2 * n * P : 2 * (n + 1) * P].bitcast(FP4X4),
-                        lhsT_scale=sk_s[:, a, :].bitcast(U8)[:, n * P : (n + 1) * P],
-                        rhs=rhs,
-                        rhs_scale=rhs_scale,
-                        start=(a == 0),
-                        stop=False,
-                    )
+        def sketch(acc, n, j0, j1, start, stop):
+            step = 512 if j1 - j0 == 512 else 128
+            todo = [(g0, a) for g0 in range(j0, j1, step) for a in range(PASSES)]
+            for i, (g0, a) in enumerate(todo):
+                rhs, rhs_scale = doc_operand(a, g0, g0 + step)
                 nc.tensor.matmul_mx(
-                    out=acc,
-                    lhsT=dec_w[:, n * P : (n + 1) * P].bitcast(FP8X4),
-                    lhsT_scale=dec_s[:, n * P : (n + 1) * P],
-                    rhs=code_w[:, g0 : g0 + step].bitcast(FP8X4),
-                    rhs_scale=code_s[:, g0 : g0 + step],
-                    start=False,
-                    stop=True,
+                    out=acc[:, g0 - j0 : g0 - j0 + step],
+                    lhsT=sk_w[:, a, :].bitcast(U8)[:, 2 * n * P : 2 * (n + 1) * P].bitcast(FP4X4),
+                    lhsT_scale=sk_s[:, a, :].bitcast(U8)[:, n * P : (n + 1) * P],
+                    rhs=rhs,
+                    rhs_scale=rhs_scale,
+                    start=(start and i == 0),
+                    stop=(stop and i == len(todo) - 1),
                 )
-            nc.scalar.activation(dst, bank[:, 0:width], ACT.Abs)
 
-        def scatter(n, j0, j1, span=512):
-            size = ring.tile([P, S], F32, name="size")
-            for g0 in range(j0, j1, span):
-                g1 = min(g0 + span, j1)
-                residual(n, g0, g1, size[:, g0 - j0 : g1 - j0])
+        def decode(acc, n, j0, j1, start, stop):
+            nc.tensor.matmul_mx(
+                out=acc[:, 0 : j1 - j0],
+                lhsT=dec_w[:, n * P : (n + 1) * P].bitcast(FP8X4),
+                lhsT_scale=dec_s[:, n * P : (n + 1) * P],
+                rhs=code_w[:, j0:j1].bitcast(FP8X4),
+                rhs_scale=code_s[:, j0:j1],
+                start=start,
+                stop=stop,
+            )
+
+        def residual(b, n, j0, j1, sketch_first, dst):
+            acc = bank(b)
+            if sketch_first:
+                sketch(acc, n, j0, j1, True, False)
+                decode(acc, n, j0, j1, False, True)
+            else:
+                decode(acc, n, j0, j1, True, False)
+                sketch(acc, n, j0, j1, False, True)
+            nc.scalar.activation(dst, acc[:, 0 : j1 - j0], ACT.Abs)
+
+        def sized(n, j0, j1, tag):
+            size[n, j0] = keep.tile([P, j1 - j0], F32, name="size%d_%d" % (n, j0), tag=tag, align_bytes=64)
+            return size[n, j0][:]
+
+        def scatter(n, j0, j1):
             window = cache[n % CACHE_BUFS]
             nc.vector.tensor_tensor(
-                window[:].indirect(place[:, j0 // 16 : j1 // 16]), size[:, 0 : j1 - j0], weight[:, j0:j1], ALU.mult
+                window[:].indirect(place[:, j0 // 16 : j1 // 16]), size[n, j0][:], weight[:, j0:j1], ALU.mult
             )
             if j1 == S:
                 nc.sync.dma_start(out[n * P : (n + 1) * P, :], window[:])
 
         last = PASSES - 1
-        gather_words(0, 0, S)
-        load_table(last)
+        load_enc(0)
+        nc.sync.dma_start(pick[:], offs)
+        for a in range(PASSES):
+            nc.sync.dma_start(tab_s[16 + a : 64 : PASSES, :], tab_scales[a].bitcast(I32))
+        nc.vector.memset(tab_s[0:16, :], 0)
+        nc.vector.memset(tab_s[64:128, :], 0)
+        for b in range(CACHE_BUFS):
+            nc.gpsimd.memset(cache[b][:], 0.0)
+        load_table(0)
+        load_enc(1)
+        load_table(1)
+        nc.sync.dma_start(place[:], offs2)
+        nc.vector.memset(doc_s[:], 0)
+        nc.vector.memset(sk_s[:], 0)
+
+        nc.vector.tensor_copy(doc_s_rows[:], tab_s[:].bitcast(U8).indirect(pick[:]))
+        nc.gpsimd.dma_start(bias[:], benc.rearrange("(p t) -> p t", t=4))
+        for q in range(4):
+            nc.gpsimd.dma_start(
+                sk_s[32 * q : 32 * q + 4, :, :],
+                wsk_scales[:, 4 * q : 4 * q + 4, :].bitcast(I32).rearrange("a r n -> r a n"),
+            )
+
         cast_enc(nc.scalar.copy, 0, 0, P)
-        load_dec(0)
+        load_enc(last)
+        gather_words(0, 0, S)
+        load_dec(0, 128)
+        for q in range(4):
+            nc.sync.dma_start(
+                doc_s[32 * q : 32 * q + 4, :, :], doc_s_rows[16 + 12 * q : 28 + 12 * q, :].bitcast(I32)
+            )
+        quant_enc(0)
         cast_enc(nc.scalar.copy, 1, 0, P)
-        sk_w = staged([P, PASSES, 2 * N // 4], I32, "sk_w")
-        nc.sync.dma_start(sk_w[:], wsk_words.bitcast(I32).rearrange("a p c -> p a c"))
-        quant_enc(0, 0, 4)
+        load_table(last)
         gather_words(1, 0, S)
-        weight = staged([P, S], F32, "weight")
-        nc.sync.dma_start(weight[:, 0:256], wgo[:, 0:256])
-        quant_enc(1, 0, 4)
+        load_dec(128, 256)
+        quant_enc(1)
         cast_enc(nc.scalar.copy, last, 0, 64)
         cast_enc(nc.vector.tensor_copy, last, 64, P)
-        load_dec(1)
-        nc.sync.dma_start(weight[:, 256:S], wgo[:, 256:S])
-        quant_enc(last, 0, 4)
-        gather_words(last, 0, 256)
-        gather_words(last, 256, S)
-        load_dec(2)
-        cast_dec(0, 128, True)
+        sk_w = staged([P, PASSES, 2 * N // 4], I32, "sk_w")
+        nc.sync.dma_start(sk_w[:], wsk_words.bitcast(I32).rearrange("a p c -> p a c"))
+        quant_enc(last)
+        cast_dec(0, 0, 128)
+        weight = staged([P, S], F32, "weight")
+        nc.sync.dma_start(weight[:], wgo)
         quant_dec(0, 128)
 
-        encode(0, 256, nc.vector.tensor_copy)
-        scatter(0, 0, 256, 128)
-        cast_dec(128, 256, False)
+        first = [(bank(0), (0, 1), 0, 256), (bank(1), (2, 3), 0, 256)]
+        second = [(bank(2), (0, 1), 256, 512), (bank(3), (2, 3), 256, 512)]
+        third = [(bank(6), (0,), 512, S), (bank(7), (1,), 512, S)]
+        for a in range(last):
+            for acc, ts, j0, j1 in first + second + third:
+                encode_pass(acc, ts, a, j0, j1)
+
+        gather_words(last, 0, 256)
+        gather_words(last, 256, 512)
+        gather_words(last, 512, S)
+        for acc, ts, j0, j1 in first:
+            encode_pass(acc, ts, last, j0, j1)
+            relu(acc, ts, j0, j1)
+        interleave(nc.vector.tensor_copy, 0, 256)
+        quant_code(0, 256)
+        residual(4, 0, 0, 256, True, sized(0, 0, 256, "size_a0"))
+        cast_dec(128, 128, 256)
+        load_dec(256, N)
         quant_dec(128, 256)
+        for acc, ts, j0, j1 in second:
+            encode_pass(acc, ts, last, j0, j1)
+            relu(acc, ts, j0, j1)
+        scatter(0, 0, 256)
+        interleave(nc.vector.tensor_copy, 256, 512)
+        quant_code(256, 512)
+        residual(5, 1, 0, 256, True, sized(1, 0, 256, "size_a1"))
+        for acc, ts, j0, j1 in third:
+            encode_pass(acc, ts, last, j0, j1)
+            relu(acc, ts, j0, j1)
         scatter(1, 0, 256)
-        cast_dec(256, 512, False)
-        quant_dec(256, 512)
-        encode(256, 512, nc.scalar.copy)
-        scatter(2, 0, 256)
-        scatter(3, 0, 256)
+        for b, t in ((2, 2), (3, 3)):
+            acc = bank(b)
+            for a in range(PASSES):
+                encode_pass(acc, (t,), a, 512, S)
+            relu(acc, (t,), 512, S)
+        interleave(nc.scalar.copy, 512, 768)
+        quant_code(512, 768)
+        residual(0, 0, 256, 512, False, sized(0, 256, 512, "planes512"))
         scatter(0, 256, 512)
-        encode(512, 1024, nc.scalar.copy)
-        for n in range(1, CACHE_BUFS):
-            scatter(n, 256, 512)
-        cast_dec(512, 768, False)
-        quant_dec(512, 768)
-        for n in range(CACHE_BUFS):
-            scatter(n, 512, 1024)
-        for n in range(CACHE_BUFS, ROW_TILES):
-            scatter(n, 0, 1024)
+        interleave(nc.scalar.copy, 768, S)
+        quant_code(768, S)
+        residual(1, 1, 256, 512, False, sized(1, 256, 512, "planes768"))
+        scatter(1, 256, 512)
+        cast_dec(256, 256, 512)
+        quant_dec(256, 512)
+        residual(4, 0, 512, S, True, sized(0, 512, S, "size_c0"))
+        scatter(0, 512, S)
+        cast_dec(256, 512, N)
+        quant_dec(512, N)
+        residual(5, 1, 512, S, True, sized(1, 512, S, "size_c1"))
+        scatter(1, 512, S)
+        for n in range(2, ROW_TILES):
+            whole = sized(n, 0, S, "size%d" % n)
+            for half in range(2):
+                j0 = 512 * half
+                residual((2 * n + half + 2) % 8, n, j0, j0 + 512, True, whole[:, j0 : j0 + 512])
+            scatter(n, 0, S)

@@ -208,6 +208,10 @@ def tile_list_shortlist_coding_residual_kernel(
         nc.vector.memset(sk_s[:], 0)
 
         nc.vector.tensor_copy(doc_s_rows[:], tab_s[:].bitcast(U8).indirect(pick[:]))
+        for q in range(4):
+            (nc.sync, nc.scalar)[q % 2].dma_start(
+                doc_s[32 * q : 32 * q + 4, :, :], doc_s_rows[16 + 12 * q : 28 + 12 * q, :].bitcast(I32)
+            )
         nc.gpsimd.dma_start(bias[:], benc.rearrange("(p t) -> p t", t=4))
         for q in range(4):
             nc.gpsimd.dma_start(
@@ -218,14 +222,10 @@ def tile_list_shortlist_coding_residual_kernel(
         cast_enc(nc.scalar.copy, 0, 0, P)
         load_enc(last)
         gather_words(0, 0, S)
-        load_dec(0, 128)
-        for q in range(4):
-            nc.sync.dma_start(
-                doc_s[32 * q : 32 * q + 4, :, :], doc_s_rows[16 + 12 * q : 28 + 12 * q, :].bitcast(I32)
-            )
+        load_table(last)
         quant_enc(0)
         cast_enc(nc.scalar.copy, 1, 0, P)
-        load_table(last)
+        load_dec(0, 128)
         gather_words(1, 0, S)
         load_dec(128, 256)
         quant_enc(1)

@@ -18,8 +18,8 @@ ALU = mybir.AluOpType
 
 PASSES = K // 512
 ROW_TILES = N // P
-STAGED_BUFS = 4
-CACHE_BUFS = 2
+SLOT = 8192
+CACHE_BUFS = 3
 
 
 def tile_list_shortlist_coding_residual_kernel(
@@ -28,7 +28,7 @@ def tile_list_shortlist_coding_residual_kernel(
     nc = tc.nc
     with ExitStack() as ctx:
         keep = ctx.enter_context(tc.tile_pool(name="keep", bufs=1))
-        stage = ctx.enter_context(tc.tile_pool(name="stage", bufs=STAGED_BUFS))
+        stage = ctx.enter_context(tc.tile_pool(name="stage", bufs=1))
         psum = ctx.enter_context(tc.psum_pool(name="psum", bufs=1))
 
         pick = keep.tile([P, S // 16], U16, name="pick")
@@ -51,25 +51,31 @@ def tile_list_shortlist_coding_residual_kernel(
         planes, size = {}, {}
         cache = [keep.tile([P, T2], F32, name="cache%d" % b) for b in range(CACHE_BUFS)]
 
-        def staged(shape, dtype, name):
-            return stage.tile(shape, dtype, name=name, tag="staged", align_bytes=64)
+        def staged(shape, dtype, name, offset):
+            return stage.tile(shape, dtype, name=name, offset=offset, align_bytes=64)
 
         def bank(b):
             return psum.tile([P, 512], F32, name="bank%d" % b, tag="bank%d" % b)
 
-        tab_w, enc_raw, dec_raw = {}, {}, {}
+        tab_w, enc_raw, dec_raw, sk_w = {}, {}, {}, {}
 
-        def load_table(a):
-            tab_w[a] = staged([P, T], I32, "tab_w%d" % a)
+        def load_table(a, offset):
+            tab_w[a] = staged([P, T], I32, "tab_w%d" % a, offset)
             nc.sync.dma_start(tab_w[a][:], tab_words[a].rearrange("p t i -> p (t i)").bitcast(I32))
 
-        def load_enc(a):
-            enc_raw[a] = staged([P, 4, H], F32, "enc_raw%d" % a)
+        def load_enc(a, offset):
+            enc_raw[a] = staged([P, 4, H], F32, "enc_raw%d" % a, offset)
             nc.sync.dma_start(enc_raw[a][:], wenc[512 * a : 512 * (a + 1), :].rearrange("(p j) c -> p j c", j=4))
 
-        def load_dec(c0, c1):
-            dec_raw[c0] = staged([P, 4, c1 - c0], F32, "dec_raw%d" % c0)
+        def load_dec(c0, c1, offset):
+            dec_raw[c0] = staged([P, 4, c1 - c0], F32, "dec_raw%d" % c0, offset)
             nc.sync.dma_start(dec_raw[c0][:], wdec.rearrange("(p j) n -> p j n", j=4)[:, :, c0:c1])
+
+        def load_sketch(n0, n1, offset):
+            words = staged([P, PASSES, 64 * (n1 - n0)], I32, "sk_w%d" % n0, offset)
+            nc.sync.dma_start(words[:], wsk_words.bitcast(I32).rearrange("a p c -> p a c")[:, :, 64 * n0 : 64 * n1])
+            for n in range(n0, n1):
+                sk_w[n] = words[:, :, 64 * (n - n0) : 64 * (n - n0 + 1)]
 
         def gather_words(a, j0, j1):
             nc.vector.tensor_copy(doc_w[a][:, j0:j1], tab_w[a][:].bitcast(U32).indirect(pick[:, j0 // 16 : j1 // 16]))
@@ -150,7 +156,7 @@ def tile_list_shortlist_coding_residual_kernel(
                 rhs, rhs_scale = doc_operand(a, g0, g0 + step)
                 nc.tensor.matmul_mx(
                     out=acc[:, g0 - j0 : g0 - j0 + step],
-                    lhsT=sk_w[:, a, :].bitcast(U8)[:, 2 * n * P : 2 * (n + 1) * P].bitcast(FP4X4),
+                    lhsT=sk_w[n][:, a, :].bitcast(U8).bitcast(FP4X4),
                     lhsT_scale=sk_s[:, a, :].bitcast(U8)[:, n * P : (n + 1) * P],
                     rhs=rhs,
                     rhs_scale=rhs_scale,
@@ -192,7 +198,7 @@ def tile_list_shortlist_coding_residual_kernel(
                 nc.sync.dma_start(out[n * P : (n + 1) * P, :], window[:])
 
         last = PASSES - 1
-        load_enc(0)
+        load_enc(0, 0)
         nc.sync.dma_start(pick[:], offs)
         for a in range(PASSES):
             nc.sync.dma_start(tab_s[16 + a : 64 : PASSES, :], tab_scales[a].bitcast(I32))
@@ -200,9 +206,9 @@ def tile_list_shortlist_coding_residual_kernel(
         nc.vector.memset(tab_s[64:128, :], 0)
         for b in range(CACHE_BUFS):
             nc.gpsimd.memset(cache[b][:], 0.0)
-        load_table(0)
-        load_enc(1)
-        load_table(1)
+        load_table(0, SLOT)
+        load_enc(1, 2 * SLOT)
+        load_table(1, 3 * SLOT)
         nc.sync.dma_start(place[:], offs2)
         nc.vector.memset(doc_s[:], 0)
         nc.vector.memset(sk_s[:], 0)
@@ -220,23 +226,25 @@ def tile_list_shortlist_coding_residual_kernel(
             )
 
         cast_enc(nc.scalar.copy, 0, 0, P)
-        load_enc(last)
+        load_enc(last, 0)
         gather_words(0, 0, S)
-        load_table(last)
+        load_table(last, SLOT)
         quant_enc(0)
         cast_enc(nc.scalar.copy, 1, 0, P)
-        load_dec(0, 128)
+        load_dec(0, 128, 2 * SLOT)
+        load_sketch(0, 2, 2 * SLOT + 2048)
+        weight = staged([P, S], F32, "weight", 2 * SLOT + 4096)
+        nc.sync.dma_start(weight[:, 0:256], wgo[:, 0:256])
         gather_words(1, 0, S)
-        load_dec(128, 256)
+        load_dec(128, 256, 3 * SLOT)
+        nc.sync.dma_start(weight[:, 256:S], wgo[:, 256:S])
+        load_sketch(2, ROW_TILES, 3 * SLOT + 2048)
         quant_enc(1)
         cast_enc(nc.scalar.copy, last, 0, 64)
         cast_enc(nc.vector.tensor_copy, last, 64, P)
-        sk_w = staged([P, PASSES, 2 * N // 4], I32, "sk_w")
-        nc.sync.dma_start(sk_w[:], wsk_words.bitcast(I32).rearrange("a p c -> p a c"))
+        load_dec(256, N, 0)
         quant_enc(last)
         cast_dec(0, 0, 128)
-        weight = staged([P, S], F32, "weight")
-        nc.sync.dma_start(weight[:], wgo)
         quant_dec(0, 128)
 
         first = [(bank(0), (0, 1), 0, 256), (bank(1), (2, 3), 0, 256)]
@@ -256,7 +264,6 @@ def tile_list_shortlist_coding_residual_kernel(
         quant_code(0, 256)
         residual(4, 0, 0, 256, True, sized(0, 0, 256, "size_a0"))
         cast_dec(128, 128, 256)
-        load_dec(256, N)
         quant_dec(128, 256)
         for acc, ts, j0, j1 in second:
             encode_pass(acc, ts, last, j0, j1)

@@ -49,7 +49,7 @@ def tile_list_shortlist_coding_residual_kernel(
         code_w = keep.tile([P, S], U32, name="code_w", align_bytes=64)
         code_s = keep.tile([P, S], U8, name="code_s", align_bytes=64)
         planes, size = {}, {}
-        cache = [keep.tile([P, T2], F32, name="cache%d" % b) for b in range(CACHE_BUFS)]
+        cache = [keep.tile([P, T2], F32, name="cache%d" % b) for b in range(CACHE_BUFS - 1)]
 
         def staged(shape, dtype, name, offset):
             return stage.tile(shape, dtype, name=name, offset=offset, align_bytes=64)
@@ -204,8 +204,7 @@ def tile_list_shortlist_coding_residual_kernel(
             nc.sync.dma_start(tab_s[16 + a : 64 : PASSES, :], tab_scales[a].bitcast(I32))
         nc.vector.memset(tab_s[0:16, :], 0)
         nc.vector.memset(tab_s[64:128, :], 0)
-        for b in range(CACHE_BUFS):
-            nc.gpsimd.memset(cache[b][:], 0.0)
+        nc.gpsimd.memset(cache[1][:], 0.0)
         load_table(0, SLOT)
         load_enc(1, 2 * SLOT)
         load_table(1, 3 * SLOT)
@@ -240,12 +239,13 @@ def tile_list_shortlist_coding_residual_kernel(
         nc.sync.dma_start(weight[:, 256:S], wgo[:, 256:S])
         load_sketch(2, ROW_TILES, 3 * SLOT + 2048)
         quant_enc(1)
-        cast_enc(nc.scalar.copy, last, 0, 64)
-        cast_enc(nc.vector.tensor_copy, last, 64, P)
+        cast_enc(nc.scalar.copy, last, 0, 48)
+        cast_enc(nc.vector.tensor_copy, last, 48, P)
         load_dec(256, N, 0)
         quant_enc(last)
         cast_dec(0, 0, 128)
         quant_dec(0, 128)
+        nc.vector.memset(cache[0][:].bitcast(I32), 0)
 
         first = [(bank(0), (0, 1), 0, 256), (bank(1), (2, 3), 0, 256)]
         second = [(bank(2), (0, 1), 256, 512), (bank(3), (2, 3), 256, 512)]
@@ -289,6 +289,8 @@ def tile_list_shortlist_coding_residual_kernel(
         quant_code(768, S)
         residual(1, 1, 256, 512, False, sized(1, 256, 512, "planes768"))
         scatter(1, 256, 512)
+        cache.append(keep.tile([P, T2], F32, name="cache2", tag="planes768", align_bytes=64))
+        nc.gpsimd.memset(cache[2][:], 0.0)
         cast_dec(256, 256, 512)
         quant_dec(256, 512)
         residual(4, 0, 512, S, True, sized(0, 512, S, "size_c0"))

@@ -37,14 +37,16 @@ def tile_list_shortlist_coding_residual_kernel(
         doc_w = [keep.tile([P, S], U32, name="doc_w%d" % a, align_bytes=64) for a in range(PASSES)]
         doc_s_rows = keep.tile([P, S], U8, name="doc_s_rows", align_bytes=64)
         doc_s = keep.tile([P, PASSES, S // 4], I32, name="doc_s", align_bytes=64)
-        enc_bf = [keep.tile([P, 4, P, 4], BF16, name="enc_bf%d" % a, align_bytes=64) for a in range(PASSES)]
+        enc_bf = [
+            stage.tile([P, 4, P, 4], BF16, name="enc_bf%d" % a, offset=4 * SLOT + 5120 * a, align_bytes=64)
+            for a in range(PASSES)
+        ]
         enc_w = [keep.tile([P, H], U32, name="enc_w%d" % a, align_bytes=64) for a in range(PASSES)]
         enc_s = [keep.tile([P, H], U8, name="enc_s%d" % a, align_bytes=64) for a in range(PASSES)]
         bias = keep.tile([P, 4], F32, name="bias")
         dec_bf = keep.tile([P, N, 4], BF16, name="dec_bf", align_bytes=64)
         dec_w = keep.tile([P, N], U32, name="dec_w", align_bytes=64)
         dec_s = keep.tile([P, N], U8, name="dec_s", align_bytes=64)
-        sk_s = keep.tile([P, PASSES, N // 4], I32, name="sk_s", align_bytes=64)
         code_bf = keep.tile([P, S, 4], BF16, name="code_bf", align_bytes=64)
         code_w = keep.tile([P, S], U32, name="code_w", align_bytes=64)
         code_s = keep.tile([P, S], U8, name="code_s", align_bytes=64)
@@ -210,7 +212,6 @@ def tile_list_shortlist_coding_residual_kernel(
         load_table(1, 3 * SLOT)
         nc.sync.dma_start(place[:], offs2)
         nc.vector.memset(doc_s[:], 0)
-        nc.vector.memset(sk_s[:], 0)
 
         nc.vector.tensor_copy(doc_s_rows[:], tab_s[:].bitcast(U8).indirect(pick[:]))
         for q in range(4):
@@ -218,26 +219,27 @@ def tile_list_shortlist_coding_residual_kernel(
                 doc_s[32 * q : 32 * q + 4, :, :], doc_s_rows[16 + 12 * q : 28 + 12 * q, :].bitcast(I32)
             )
         nc.gpsimd.dma_start(bias[:], benc.rearrange("(p t) -> p t", t=4))
-        for q in range(4):
-            nc.gpsimd.dma_start(
-                sk_s[32 * q : 32 * q + 4, :, :],
-                wsk_scales[:, 4 * q : 4 * q + 4, :].bitcast(I32).rearrange("a r n -> r a n"),
-            )
 
         cast_enc(nc.scalar.copy, 0, 0, P)
         load_enc(last, 0)
         gather_words(0, 0, S)
         load_table(last, SLOT)
         quant_enc(0)
+        load_dec(0, 128, 4 * SLOT)
+        sk_s = staged([P, PASSES, N // 4], I32, "sk_s", 4 * SLOT + 2048)
+        nc.vector.memset(sk_s[:], 0)
+        for q in range(4):
+            nc.sync.dma_start(
+                sk_s[32 * q : 32 * q + 4, :, :],
+                wsk_scales[:, 4 * q : 4 * q + 4, :].bitcast(I32).rearrange("a r n -> r a n"),
+            )
         cast_enc(nc.scalar.copy, 1, 0, P)
-        load_dec(0, 128, 2 * SLOT)
-        load_sketch(0, 2, 2 * SLOT + 2048)
+        load_sketch(0, 2, 2 * SLOT)
+        load_dec(128, 256, 2 * SLOT + 2048)
         weight = staged([P, S], F32, "weight", 2 * SLOT + 4096)
-        nc.sync.dma_start(weight[:, 0:256], wgo[:, 0:256])
+        nc.sync.dma_start(weight[:], wgo)
         gather_words(1, 0, S)
-        load_dec(128, 256, 3 * SLOT)
-        nc.sync.dma_start(weight[:, 256:S], wgo[:, 256:S])
-        load_sketch(2, ROW_TILES, 3 * SLOT + 2048)
+        load_sketch(2, ROW_TILES, 3 * SLOT)
         quant_enc(1)
         cast_enc(nc.scalar.copy, last, 0, 48)
         cast_enc(nc.vector.tensor_copy, last, 48, P)

@@ -95,13 +95,13 @@ def tile_list_shortlist_coding_residual_kernel(
                 in_=enc_bf[a][:].rearrange("p t m j -> p (t m j)"),
             )
 
-        def cast_dec(d, c0, c1):
-            nc.scalar.activation(
-                dec_bf[:, c0:c1, :].rearrange("p (c i) j -> p c j i", i=4),
-                dec_raw[d][:, :, c0 - d : c1 - d].rearrange("p j (c i) -> p c j i", i=4),
-                ACT.Copy,
-                scale=-1.0,
-            )
+        def cast_dec(d, c0, c1, on_vector=False):
+            dst = dec_bf[:, c0:c1, :].rearrange("p (c i) j -> p c j i", i=4)
+            src = dec_raw[d][:, :, c0 - d : c1 - d].rearrange("p j (c i) -> p c j i", i=4)
+            if on_vector:
+                nc.vector.tensor_scalar(dst, src, -1.0, None, ALU.mult)
+            else:
+                nc.scalar.activation(dst, src, ACT.Copy, scale=-1.0)
 
         def quant_dec(c0, c1):
             nc.vector.quantize_mx(
@@ -238,9 +238,10 @@ def tile_list_shortlist_coding_residual_kernel(
         load_dec(128, 256, 2 * SLOT + 2048)
         weight = staged([P, S], F32, "weight", 2 * SLOT + 4096)
         nc.sync.dma_start(weight[:], wgo)
-        gather_words(1, 0, S)
-        load_sketch(2, ROW_TILES, 3 * SLOT)
+        gather_words(1, 0, 512)
         quant_enc(1)
+        gather_words(1, 512, S)
+        load_sketch(2, ROW_TILES, 3 * SLOT)
         cast_enc(nc.scalar.copy, last, 0, 48)
         cast_enc(nc.vector.tensor_copy, last, 48, P)
         load_dec(256, N, 0)
@@ -265,7 +266,7 @@ def tile_list_shortlist_coding_residual_kernel(
         interleave(nc.vector.tensor_copy, 0, 256)
         quant_code(0, 256)
         residual(4, 0, 0, 256, True, sized(0, 0, 256, "size_a0"))
-        cast_dec(128, 128, 256)
+        cast_dec(128, 128, 256, True)
         quant_dec(128, 256)
         for acc, ts, j0, j1 in second:
             encode_pass(acc, ts, last, j0, j1)

@@ -20,6 +20,7 @@ PASSES = K // 512
 ROW_TILES = N // P
 SLOT = 8192
 CACHE_BUFS = 3
+SCALE_ROW0 = 36
 
 
 def tile_list_shortlist_coding_residual_kernel(
@@ -37,10 +38,8 @@ def tile_list_shortlist_coding_residual_kernel(
         doc_w = [keep.tile([P, S], U32, name="doc_w%d" % a, align_bytes=64) for a in range(PASSES)]
         doc_s_rows = keep.tile([P, S], U8, name="doc_s_rows", align_bytes=64)
         doc_s = keep.tile([P, PASSES, S // 4], I32, name="doc_s", align_bytes=64)
-        enc_bf = [
-            stage.tile([P, 4, P, 4], BF16, name="enc_bf%d" % a, offset=4 * SLOT + 5120 * a, align_bytes=64)
-            for a in range(PASSES)
-        ]
+        enc_bf = [keep.tile([P, 4, P, 4], BF16, name="enc_bf%d" % a, align_bytes=64) for a in range(PASSES)]
+        weight = keep.tile([P, S], F32, name="weight", align_bytes=64)
         enc_w = [keep.tile([P, H], U32, name="enc_w%d" % a, align_bytes=64) for a in range(PASSES)]
         enc_s = [keep.tile([P, H], U8, name="enc_s%d" % a, align_bytes=64) for a in range(PASSES)]
         bias = keep.tile([P, 4], F32, name="bias")
@@ -59,7 +58,7 @@ def tile_list_shortlist_coding_residual_kernel(
         def bank(b):
             return psum.tile([P, 512], F32, name="bank%d" % b, tag="bank%d" % b)
 
-        tab_w, enc_raw, dec_raw, sk_w = {}, {}, {}, {}
+        tab_w, enc_raw, dec_raw, sk_w, sk_s = {}, {}, {}, {}, {}
 
         def load_table(a, offset):
             tab_w[a] = staged([P, T], I32, "tab_w%d" % a, offset)
@@ -69,12 +68,23 @@ def tile_list_shortlist_coding_residual_kernel(
             enc_raw[a] = staged([P, 4, H], F32, "enc_raw%d" % a, offset)
             nc.sync.dma_start(enc_raw[a][:], wenc[512 * a : 512 * (a + 1), :].rearrange("(p j) c -> p j c", j=4))
 
-        def load_dec(c0, c1, offset):
-            dec_raw[c0] = staged([P, 4, c1 - c0], F32, "dec_raw%d" % c0, offset)
+        def load_dec(c0, c1):
+            dec_raw[c0] = keep.tile([P, 4, c1 - c0], F32, name="dec_raw%d" % c0, tag="dec_raw%d" % c0, align_bytes=64)
             nc.sync.dma_start(dec_raw[c0][:], wdec.rearrange("(p j) n -> p j n", j=4)[:, :, c0:c1])
 
-        def load_sketch(n0, n1, offset):
-            words = staged([P, PASSES, 64 * (n1 - n0)], I32, "sk_w%d" % n0, offset)
+        def load_sketch_scales(n0, n1):
+            rows = keep.tile([P, PASSES, 32 * (n1 - n0)], I32, name="sk_s%d" % n0, align_bytes=64)
+            nc.vector.memset(rows[:], 0)
+            for r in range(4):
+                nc.sync.dma_start(
+                    rows[r:P:32, :, :],
+                    wsk_scales[:, r:16:4, :].bitcast(I32).rearrange("a q n -> q a n")[:, :, 32 * n0 : 32 * n1],
+                )
+            for n in range(n0, n1):
+                sk_s[n] = rows[:, :, 32 * (n - n0) : 32 * (n - n0 + 1)]
+
+        def load_sketch(n0, n1):
+            words = keep.tile([P, PASSES, 64 * (n1 - n0)], I32, name="sk_w%d" % n0, align_bytes=64)
             nc.sync.dma_start(words[:], wsk_words.bitcast(I32).rearrange("a p c -> p a c")[:, :, 64 * n0 : 64 * n1])
             for n in range(n0, n1):
                 sk_w[n] = words[:, :, 64 * (n - n0) : 64 * (n - n0 + 1)]
@@ -159,7 +169,7 @@ def tile_list_shortlist_coding_residual_kernel(
                 nc.tensor.matmul_mx(
                     out=acc[:, g0 - j0 : g0 - j0 + step],
                     lhsT=sk_w[n][:, a, :].bitcast(U8).bitcast(FP4X4),
-                    lhsT_scale=sk_s[:, a, :].bitcast(U8)[:, n * P : (n + 1) * P],
+                    lhsT_scale=sk_s[n][:, a, :].bitcast(U8),
                     rhs=rhs,
                     rhs_scale=rhs_scale,
                     start=(start and i == 0),
@@ -200,55 +210,48 @@ def tile_list_shortlist_coding_residual_kernel(
                 nc.sync.dma_start(out[n * P : (n + 1) * P, :], window[:])
 
         last = PASSES - 1
+        nc.gpsimd.memset(tab_s[:], 0)
         load_enc(0, 0)
         nc.sync.dma_start(pick[:], offs)
         for a in range(PASSES):
-            nc.sync.dma_start(tab_s[16 + a : 64 : PASSES, :], tab_scales[a].bitcast(I32))
-        nc.vector.memset(tab_s[0:16, :], 0)
-        nc.vector.memset(tab_s[64:128, :], 0)
-        nc.gpsimd.memset(cache[1][:], 0.0)
-        load_table(0, SLOT)
-        load_enc(1, 2 * SLOT)
-        load_table(1, 3 * SLOT)
-        nc.sync.dma_start(place[:], offs2)
+            row0 = SCALE_ROW0 + 4 * a
+            nc.sync.dma_start(tab_s[row0 : row0 + 46 : 3, :], tab_scales[a].bitcast(I32))
+        nc.gpsimd.dma_start(bias[:], benc.rearrange("(p t) -> p t", t=4))
         nc.vector.memset(doc_s[:], 0)
+        for window in cache:
+            nc.vector.memset(window[:].bitcast(I32), 0)
+        load_table(0, SLOT)
+        load_table(1, 3 * SLOT)
 
         nc.vector.tensor_copy(doc_s_rows[:], tab_s[:].bitcast(U8).indirect(pick[:]))
-        for q in range(4):
-            (nc.sync, nc.scalar)[q % 2].dma_start(
-                doc_s[32 * q : 32 * q + 4, :, :], doc_s_rows[16 + 12 * q : 28 + 12 * q, :].bitcast(I32)
-            )
-        nc.gpsimd.dma_start(bias[:], benc.rearrange("(p t) -> p t", t=4))
-
         cast_enc(nc.scalar.copy, 0, 0, P)
+        for r in range(4):
+            row0 = SCALE_ROW0 + 3 * r
+            nc.scalar.dma_start(doc_s[r:P:32, :, :], doc_s_rows[row0 : row0 + 45 : 4, :].bitcast(I32))
+        load_enc(1, 2 * SLOT)
+        nc.sync.dma_start(place[:], offs2)
         load_enc(last, 0)
+        quant_enc(0)
         gather_words(0, 0, S)
         load_table(last, SLOT)
-        quant_enc(0)
-        load_dec(0, 128, 4 * SLOT)
-        sk_s = staged([P, PASSES, N // 4], I32, "sk_s", 4 * SLOT + 2048)
-        nc.vector.memset(sk_s[:], 0)
-        for q in range(4):
-            nc.sync.dma_start(
-                sk_s[32 * q : 32 * q + 4, :, :],
-                wsk_scales[:, 4 * q : 4 * q + 4, :].bitcast(I32).rearrange("a r n -> r a n"),
-            )
-        cast_enc(nc.scalar.copy, 1, 0, P)
-        load_sketch(0, 2, 2 * SLOT)
-        load_dec(128, 256, 2 * SLOT + 2048)
-        weight = staged([P, S], F32, "weight", 2 * SLOT + 4096)
+        load_dec(0, 128)
+        load_sketch_scales(0, 2)
+        load_sketch(0, 2)
+        load_dec(128, 256)
         nc.sync.dma_start(weight[:], wgo)
-        gather_words(1, 0, 512)
+        load_dec(256, 512)
+        load_sketch(2, ROW_TILES)
+        load_sketch_scales(2, ROW_TILES)
+        load_dec(512, N)
+        gather_words(1, 0, S)
+        cast_enc(nc.scalar.copy, 1, 0, 64)
+        cast_enc(nc.vector.tensor_copy, 1, 64, P)
         quant_enc(1)
-        gather_words(1, 512, S)
-        load_sketch(2, ROW_TILES, 3 * SLOT)
         cast_enc(nc.scalar.copy, last, 0, 48)
         cast_enc(nc.vector.tensor_copy, last, 48, P)
-        load_dec(256, N, 0)
         quant_enc(last)
         cast_dec(0, 0, 128)
         quant_dec(0, 128)
-        nc.vector.memset(cache[0][:].bitcast(I32), 0)
 
         first = [(bank(0), (0, 1), 0, 256), (bank(1), (2, 3), 0, 256)]
         second = [(bank(2), (0, 1), 256, 512), (bank(3), (2, 3), 256, 512)]
@@ -296,11 +299,11 @@ def tile_list_shortlist_coding_residual_kernel(
         nc.gpsimd.memset(cache[2][:], 0.0)
         cast_dec(256, 256, 512)
         quant_dec(256, 512)
-        residual(4, 0, 512, S, True, sized(0, 512, S, "size_c0"))
+        residual(4, 0, 512, S, True, sized(0, 512, S, "dec_raw256"))
         scatter(0, 512, S)
-        cast_dec(256, 512, N)
+        cast_dec(512, 512, N)
         quant_dec(512, N)
-        residual(5, 1, 512, S, True, sized(1, 512, S, "size_c1"))
+        residual(5, 1, 512, S, True, sized(1, 512, S, "dec_raw512"))
         scatter(1, 512, S)
         for n in range(2, ROW_TILES):
             whole = sized(n, 0, S, "size%d" % n)

@@ -34,7 +34,6 @@ def tile_list_shortlist_coding_residual_kernel(
 
         pick = keep.tile([P, S // 16], U16, name="pick")
         place = keep.tile([P, S // 16], U16, name="place")
-        tab_s = keep.tile([P, T // 4], I32, name="tab_s", align_bytes=64)
         doc_w = [keep.tile([P, S], U32, name="doc_w%d" % a, align_bytes=64) for a in range(PASSES)]
         doc_s_rows = keep.tile([P, S], U8, name="doc_s_rows", align_bytes=64)
         doc_s = keep.tile([P, PASSES, S // 4], I32, name="doc_s", align_bytes=64)
@@ -50,7 +49,7 @@ def tile_list_shortlist_coding_residual_kernel(
         code_w = keep.tile([P, S], U32, name="code_w", align_bytes=64)
         code_s = keep.tile([P, S], U8, name="code_s", align_bytes=64)
         planes, size = {}, {}
-        cache = [keep.tile([P, T2], F32, name="cache%d" % b) for b in range(CACHE_BUFS - 1)]
+        cache = [keep.tile([P, T2], F32, name="cache0")]
 
         def staged(shape, dtype, name, offset):
             return stage.tile(shape, dtype, name=name, offset=offset, align_bytes=64)
@@ -210,26 +209,28 @@ def tile_list_shortlist_coding_residual_kernel(
                 nc.sync.dma_start(out[n * P : (n + 1) * P, :], window[:])
 
         last = PASSES - 1
+        tab_s = staged([P, T // 4], I32, "tab_s", 4 * SLOT)
         nc.gpsimd.memset(tab_s[:], 0)
-        load_enc(0, 0)
         nc.sync.dma_start(pick[:], offs)
+        nc.sync.dma_start(place[:], offs2)
         for a in range(PASSES):
             row0 = SCALE_ROW0 + 4 * a
             nc.sync.dma_start(tab_s[row0 : row0 + 46 : 3, :], tab_scales[a].bitcast(I32))
         nc.gpsimd.dma_start(bias[:], benc.rearrange("(p t) -> p t", t=4))
         nc.vector.memset(doc_s[:], 0)
-        for window in cache:
-            nc.vector.memset(window[:].bitcast(I32), 0)
+        nc.vector.memset(cache[0][:].bitcast(I32), 0)
+        load_enc(0, 0)
         load_table(0, SLOT)
         load_table(1, 3 * SLOT)
 
         nc.vector.tensor_copy(doc_s_rows[:], tab_s[:].bitcast(U8).indirect(pick[:]))
+        cache.append(staged([P, T2], F32, "cache1", 4 * SLOT))
+        nc.vector.memset(cache[1][:].bitcast(I32), 0)
         cast_enc(nc.scalar.copy, 0, 0, P)
         for r in range(4):
             row0 = SCALE_ROW0 + 3 * r
-            nc.scalar.dma_start(doc_s[r:P:32, :, :], doc_s_rows[row0 : row0 + 45 : 4, :].bitcast(I32))
+            nc.sync.dma_start(doc_s[r:P:32, :, :], doc_s_rows[row0 : row0 + 45 : 4, :].bitcast(I32))
         load_enc(1, 2 * SLOT)
-        nc.sync.dma_start(place[:], offs2)
         load_enc(last, 0)
         quant_enc(0)
         gather_words(0, 0, S)

@@ -219,8 +219,8 @@ def tile_list_shortlist_coding_residual_kernel(
         nc.gpsimd.dma_start(bias[:], benc.rearrange("(p t) -> p t", t=4))
         nc.vector.memset(doc_s[:], 0)
         nc.vector.memset(cache[0][:].bitcast(I32), 0)
-        load_enc(0, 0)
         load_table(0, SLOT)
+        load_enc(0, 0)
         load_table(1, 3 * SLOT)
 
         nc.vector.tensor_copy(doc_s_rows[:], tab_s[:].bitcast(U8).indirect(pick[:]))
@@ -232,7 +232,6 @@ def tile_list_shortlist_coding_residual_kernel(
             nc.sync.dma_start(doc_s[r:P:32, :, :], doc_s_rows[row0 : row0 + 45 : 4, :].bitcast(I32))
         load_enc(1, 2 * SLOT)
         load_enc(last, 0)
-        quant_enc(0)
         gather_words(0, 0, S)
         load_table(last, SLOT)
         load_dec(0, 128)
@@ -244,7 +243,9 @@ def tile_list_shortlist_coding_residual_kernel(
         load_sketch(2, ROW_TILES)
         load_sketch_scales(2, ROW_TILES)
         load_dec(512, N)
-        gather_words(1, 0, S)
+        gather_words(1, 0, 512)
+        quant_enc(0)
+        gather_words(1, 512, S)
         cast_enc(nc.scalar.copy, 1, 0, 64)
         cast_enc(nc.vector.tensor_copy, 1, 64, P)
         quant_enc(1)

@@ -59,9 +59,13 @@ def tile_list_shortlist_coding_residual_kernel(
 
         tab_w, enc_raw, dec_raw, sk_w, sk_s = {}, {}, {}, {}, {}
 
+        def load_table_columns(a, t0, t1):
+            words = tab_words[a].rearrange("p t i -> p (t i)").bitcast(I32)
+            nc.sync.dma_start(tab_w[a][:, t0:t1], words[:, t0:t1])
+
         def load_table(a, offset):
             tab_w[a] = staged([P, T], I32, "tab_w%d" % a, offset)
-            nc.sync.dma_start(tab_w[a][:], tab_words[a].rearrange("p t i -> p (t i)").bitcast(I32))
+            load_table_columns(a, 0, T)
 
         def load_enc(a, offset):
             enc_raw[a] = staged([P, 4, H], F32, "enc_raw%d" % a, offset)
@@ -209,28 +213,30 @@ def tile_list_shortlist_coding_residual_kernel(
                 nc.sync.dma_start(out[n * P : (n + 1) * P, :], window[:])
 
         last = PASSES - 1
-        tab_s = staged([P, T // 4], I32, "tab_s", 4 * SLOT)
+        tab_s = keep.tile([P, T // 4], I32, name="tab_s", align_bytes=64)
         nc.gpsimd.memset(tab_s[:], 0)
+        tab_w[0] = staged([P, T], I32, "tab_w0", SLOT)
+        load_table_columns(0, 0, T // 2)
         nc.sync.dma_start(pick[:], offs)
-        nc.sync.dma_start(place[:], offs2)
         for a in range(PASSES):
             row0 = SCALE_ROW0 + 4 * a
             nc.sync.dma_start(tab_s[row0 : row0 + 46 : 3, :], tab_scales[a].bitcast(I32))
         nc.gpsimd.dma_start(bias[:], benc.rearrange("(p t) -> p t", t=4))
         nc.vector.memset(doc_s[:], 0)
-        nc.vector.memset(cache[0][:].bitcast(I32), 0)
-        load_table(0, SLOT)
+        cache.append(keep.tile([P, T2], F32, name="cache1"))
+        for window in cache:
+            nc.vector.memset(window[:].bitcast(I32), 0)
+        load_table_columns(0, T // 2, T)
         load_enc(0, 0)
         load_table(1, 3 * SLOT)
+        load_enc(1, 2 * SLOT)
 
         nc.vector.tensor_copy(doc_s_rows[:], tab_s[:].bitcast(U8).indirect(pick[:]))
-        cache.append(staged([P, T2], F32, "cache1", 4 * SLOT))
-        nc.vector.memset(cache[1][:].bitcast(I32), 0)
         cast_enc(nc.scalar.copy, 0, 0, P)
         for r in range(4):
             row0 = SCALE_ROW0 + 3 * r
             nc.sync.dma_start(doc_s[r:P:32, :, :], doc_s_rows[row0 : row0 + 45 : 4, :].bitcast(I32))
-        load_enc(1, 2 * SLOT)
+        nc.sync.dma_start(place[:], offs2)
         load_enc(last, 0)
         gather_words(0, 0, S)
         load_table(last, SLOT)

@@ -17,9 +17,11 @@ ACT = mybir.ActivationFunctionType
 ALU = mybir.AluOpType
 
 PASSES = K // 512
+LAST = PASSES - 1
 ROW_TILES = N // P
+EARLY = 2
+STRETCH = 256
 SLOT = 8192
-CACHE_BUFS = 3
 SCALE_ROW0 = 36
 
 
@@ -32,24 +34,8 @@ def tile_list_shortlist_coding_residual_kernel(
         stage = ctx.enter_context(tc.tile_pool(name="stage", bufs=1))
         psum = ctx.enter_context(tc.psum_pool(name="psum", bufs=1))
 
-        pick = keep.tile([P, S // 16], U16, name="pick")
-        place = keep.tile([P, S // 16], U16, name="place")
-        doc_w = [keep.tile([P, S], U32, name="doc_w%d" % a, align_bytes=64) for a in range(PASSES)]
-        doc_s_rows = keep.tile([P, S], U8, name="doc_s_rows", align_bytes=64)
-        doc_s = keep.tile([P, PASSES, S // 4], I32, name="doc_s", align_bytes=64)
-        enc_bf = [keep.tile([P, 4, P, 4], BF16, name="enc_bf%d" % a, align_bytes=64) for a in range(PASSES)]
-        weight = keep.tile([P, S], F32, name="weight", align_bytes=64)
-        enc_w = [keep.tile([P, H], U32, name="enc_w%d" % a, align_bytes=64) for a in range(PASSES)]
-        enc_s = [keep.tile([P, H], U8, name="enc_s%d" % a, align_bytes=64) for a in range(PASSES)]
-        bias = keep.tile([P, 4], F32, name="bias")
-        dec_bf = keep.tile([P, N, 4], BF16, name="dec_bf", align_bytes=64)
-        dec_w = keep.tile([P, N], U32, name="dec_w", align_bytes=64)
-        dec_s = keep.tile([P, N], U8, name="dec_s", align_bytes=64)
-        code_bf = keep.tile([P, S, 4], BF16, name="code_bf", align_bytes=64)
-        code_w = keep.tile([P, S], U32, name="code_w", align_bytes=64)
-        code_s = keep.tile([P, S], U8, name="code_s", align_bytes=64)
-        planes, size = {}, {}
-        cache = [keep.tile([P, T2], F32, name="cache0")]
+        def kept(shape, dtype, name, tag=None):
+            return keep.tile(shape, dtype, name=name, tag=tag or name, align_bytes=64)
 
         def staged(shape, dtype, name, offset):
             return stage.tile(shape, dtype, name=name, offset=offset, align_bytes=64)
@@ -57,7 +43,21 @@ def tile_list_shortlist_coding_residual_kernel(
         def bank(b):
             return psum.tile([P, 512], F32, name="bank%d" % b, tag="bank%d" % b)
 
-        tab_w, enc_raw, dec_raw, sk_w, sk_s = {}, {}, {}, {}, {}
+        pick = keep.tile([P, S // 16], U16, name="pick")
+        place = keep.tile([P, S // 16], U16, name="place")
+        bias = kept([P, 4], F32, "bias")
+        weight = kept([P, S], F32, "weight")
+        doc_s_rows = kept([P, S], U8, "doc_s_rows")
+        doc_s = kept([P, PASSES, S // 4], I32, "doc_s")
+        enc_bf = [kept([P, 4, P, 4], BF16, "enc_bf%d" % a) for a in range(PASSES)]
+        enc_w = [kept([P, H], U32, "enc_w%d" % a) for a in range(PASSES)]
+        enc_s = [kept([P, H], U8, "enc_s%d" % a) for a in range(PASSES)]
+        dec_w = kept([P, N], U32, "dec_w")
+        dec_s = kept([P, N], U8, "dec_s")
+        code_w = kept([P, S], U32, "code_w")
+        code_s = kept([P, S], U8, "code_s")
+        sk_s = kept([P, PASSES, N // 4], I32, "sk_s")
+        tab_w, enc_raw, dec_raw, dec_bf, sk_w, doc_w, code_bf, planes, size, cache = ({} for i in range(10))
 
         def load_table_columns(a, t0, t1):
             words = tab_words[a].rearrange("p t i -> p (t i)").bitcast(I32)
@@ -72,28 +72,26 @@ def tile_list_shortlist_coding_residual_kernel(
             nc.sync.dma_start(enc_raw[a][:], wenc[512 * a : 512 * (a + 1), :].rearrange("(p j) c -> p j c", j=4))
 
         def load_dec(c0, c1):
-            dec_raw[c0] = keep.tile([P, 4, c1 - c0], F32, name="dec_raw%d" % c0, tag="dec_raw%d" % c0, align_bytes=64)
+            dec_raw[c0] = kept([P, 4, c1 - c0], F32, "dec_raw%d" % c0)
             nc.sync.dma_start(dec_raw[c0][:], wdec.rearrange("(p j) n -> p j n", j=4)[:, :, c0:c1])
 
-        def load_sketch_scales(n0, n1):
-            rows = keep.tile([P, PASSES, 32 * (n1 - n0)], I32, name="sk_s%d" % n0, align_bytes=64)
-            nc.vector.memset(rows[:], 0)
-            for r in range(4):
-                nc.sync.dma_start(
-                    rows[r:P:32, :, :],
-                    wsk_scales[:, r:16:4, :].bitcast(I32).rearrange("a q n -> q a n")[:, :, 32 * n0 : 32 * n1],
-                )
-            for n in range(n0, n1):
-                sk_s[n] = rows[:, :, 32 * (n - n0) : 32 * (n - n0 + 1)]
-
         def load_sketch(n0, n1):
-            words = keep.tile([P, PASSES, 64 * (n1 - n0)], I32, name="sk_w%d" % n0, align_bytes=64)
+            words = kept([P, PASSES, 64 * (n1 - n0)], I32, "sk_w%d" % n0)
             nc.sync.dma_start(words[:], wsk_words.bitcast(I32).rearrange("a p c -> p a c")[:, :, 64 * n0 : 64 * n1])
             for n in range(n0, n1):
                 sk_w[n] = words[:, :, 64 * (n - n0) : 64 * (n - n0 + 1)]
 
+        def doc_tile(a, j0, j1, tag=None):
+            tile = kept([P, j1 - j0], U32, "doc_w%d_%d" % (a, j0), tag)
+            for g in range(j0, j1, P):
+                doc_w[a, g] = (tile, j0)
+
+        def doc_words(a, j0, j1):
+            tile, first = doc_w[a, j0]
+            return tile[:, j0 - first : j1 - first]
+
         def gather_words(a, j0, j1):
-            nc.vector.tensor_copy(doc_w[a][:, j0:j1], tab_w[a][:].bitcast(U32).indirect(pick[:, j0 // 16 : j1 // 16]))
+            nc.vector.tensor_copy(doc_words(a, j0, j1), tab_w[a][:].bitcast(U32).indirect(pick[:, j0 // 16 : j1 // 16]))
 
         def cast_enc(engine_copy, a, m0, m1):
             engine_copy(
@@ -108,25 +106,25 @@ def tile_list_shortlist_coding_residual_kernel(
                 in_=enc_bf[a][:].rearrange("p t m j -> p (t m j)"),
             )
 
-        def cast_dec(d, c0, c1, on_vector=False):
-            dst = dec_bf[:, c0:c1, :].rearrange("p (c i) j -> p c j i", i=4)
-            src = dec_raw[d][:, :, c0 - d : c1 - d].rearrange("p j (c i) -> p c j i", i=4)
-            if on_vector:
-                nc.vector.tensor_scalar(dst, src, -1.0, None, ALU.mult)
-            else:
-                nc.scalar.activation(dst, src, ACT.Copy, scale=-1.0)
+        def cast_dec(c0, c1):
+            nc.scalar.activation(
+                dec_bf[c0].rearrange("p (c i) j -> p c j i", i=4),
+                dec_raw[c0][:].rearrange("p j (c i) -> p c j i", i=4),
+                ACT.Copy,
+                scale=-1.0,
+            )
 
         def quant_dec(c0, c1):
             nc.vector.quantize_mx(
                 out=dec_w[:, c0:c1].bitcast(FP8X4),
                 scales=dec_s[:, c0:c1],
-                in_=dec_bf[:, c0:c1, :].rearrange("p c j -> p (c j)"),
+                in_=dec_bf[c0].rearrange("p c j -> p (c j)"),
             )
 
         def doc_operand(a, j0, j1):
-            return doc_w[a][:, j0:j1].bitcast(FP8X4), doc_s[:, a, :].bitcast(U8)[:, j0:j1]
+            return doc_words(a, j0, j1).bitcast(FP8X4), doc_s[:, a, :].bitcast(U8)[:, j0:j1]
 
-        def encode_pass(acc, ts, a, j0, j1):
+        def encode_pass(acc, ts, a, j0, j1, closes=True):
             width = j1 - j0
             rhs, rhs_scale = doc_operand(a, j0, j1)
             for u, t in enumerate(ts):
@@ -137,23 +135,34 @@ def tile_list_shortlist_coding_residual_kernel(
                     rhs=rhs,
                     rhs_scale=rhs_scale,
                     start=(a == 0 and u == 0),
-                    stop=(a == PASSES - 1 and u == len(ts) - 1),
+                    stop=(closes and a == LAST and u == len(ts) - 1),
                 )
 
-        def relu(acc, ts, j0, j1):
-            width = j1 - j0
-            for g0 in range(j0, j1, 256):
-                if g0 not in planes:
-                    planes[g0] = keep.tile([P, 4, 256], BF16, name="planes%d" % g0, tag="planes%d" % g0, align_bytes=64)
-                for u, t in enumerate(ts):
-                    c0 = u * width + g0 - j0
-                    nc.scalar.activation(
-                        planes[g0][:, t, :], acc[:, c0 : c0 + 256], ACT.Relu, bias=bias[:, t : t + 1]
-                    )
+        def add_bias(acc, j0):
+            code_bf[j0] = kept([P, P, 4], BF16, "code_bf%d" % j0)
+            nc.vector.tensor_tensor(
+                code_bf[j0][:],
+                acc[:].rearrange("p (t c) -> p c t", t=4),
+                bias[:].unsqueeze(1).to_broadcast([P, P, 4]),
+                ALU.add,
+            )
 
-        def interleave(engine_copy, j0, j1):
-            engine_copy(
-                code_bf[:, j0:j1, :].rearrange("p (c i) t -> p c t i", i=4),
+        def clip(j0):
+            flat = code_bf[j0][:].rearrange("p c t -> p (c t)")
+            nc.vector.tensor_scalar(flat, flat, 0.0, None, ALU.max)
+
+        def relu(acc, ts, j0):
+            if j0 not in planes:
+                planes[j0] = kept([P, 4, STRETCH], BF16, "planes%d" % j0)
+            for u, t in enumerate(ts):
+                nc.scalar.activation(
+                    planes[j0][:, t, :], acc[:, u * STRETCH : (u + 1) * STRETCH], ACT.Relu, bias=bias[:, t : t + 1]
+                )
+
+        def interleave(j0):
+            code_bf[j0] = kept([P, STRETCH, 4], BF16, "code_bf%d" % j0)
+            nc.scalar.copy(
+                code_bf[j0][:].rearrange("p (c i) t -> p c t i", i=4),
                 planes[j0][:].rearrange("p t (c i) -> p c t i", i=4),
             )
 
@@ -161,23 +170,26 @@ def tile_list_shortlist_coding_residual_kernel(
             nc.vector.quantize_mx(
                 out=code_w[:, j0:j1].bitcast(FP8X4),
                 scales=code_s[:, j0:j1],
-                in_=code_bf[:, j0:j1, :].rearrange("p c t -> p (c t)"),
+                in_=code_bf[j0][:].rearrange("p c t -> p (c t)"),
             )
 
         def sketch(acc, n, j0, j1, start, stop):
-            step = 512 if j1 - j0 == 512 else 128
-            todo = [(g0, a) for g0 in range(j0, j1, step) for a in range(PASSES)]
-            for i, (g0, a) in enumerate(todo):
-                rhs, rhs_scale = doc_operand(a, g0, g0 + step)
+            todo = [(a, g0, g1) for a in range(PASSES) for g0, g1 in doc_runs(a, j0, j1)]
+            for i, (a, g0, g1) in enumerate(todo):
+                rhs, rhs_scale = doc_operand(a, g0, g1)
                 nc.tensor.matmul_mx(
-                    out=acc[:, g0 - j0 : g0 - j0 + step],
+                    out=acc[:, g0 - j0 : g1 - j0],
                     lhsT=sk_w[n][:, a, :].bitcast(U8).bitcast(FP4X4),
-                    lhsT_scale=sk_s[n][:, a, :].bitcast(U8),
+                    lhsT_scale=sk_s[:, a, :].bitcast(U8)[:, n * P : (n + 1) * P],
                     rhs=rhs,
                     rhs_scale=rhs_scale,
                     start=(start and i == 0),
                     stop=(stop and i == len(todo) - 1),
                 )
+
+        def doc_runs(a, j0, j1):
+            cuts = [g for g in range(j0, j1, P) if g == j0 or doc_w[a, g][1] == g] + [j1]
+            return list(zip(cuts[:-1], cuts[1:]))
 
         def decode(acc, n, j0, j1, start, stop):
             nc.tensor.matmul_mx(
@@ -190,32 +202,30 @@ def tile_list_shortlist_coding_residual_kernel(
                 stop=stop,
             )
 
-        def residual(b, n, j0, j1, sketch_first, dst):
-            acc = bank(b)
+        def residual(acc, n, j0, j1, dst, sketch_first=True, opens=True):
             if sketch_first:
-                sketch(acc, n, j0, j1, True, False)
+                sketch(acc, n, j0, j1, opens, False)
                 decode(acc, n, j0, j1, False, True)
             else:
-                decode(acc, n, j0, j1, True, False)
+                decode(acc, n, j0, j1, opens, False)
                 sketch(acc, n, j0, j1, False, True)
             nc.scalar.activation(dst, acc[:, 0 : j1 - j0], ACT.Abs)
 
-        def sized(n, j0, j1, tag):
-            size[n, j0] = keep.tile([P, j1 - j0], F32, name="size%d_%d" % (n, j0), tag=tag, align_bytes=64)
+        def sized(n, j0, j1, tag=None):
+            size[n, j0] = kept([P, j1 - j0], F32, "size%d_%d" % (n, j0), tag)
             return size[n, j0][:]
 
         def scatter(n, j0, j1):
-            window = cache[n % CACHE_BUFS]
+            window = cache[n % 3]
             nc.vector.tensor_tensor(
                 window[:].indirect(place[:, j0 // 16 : j1 // 16]), size[n, j0][:], weight[:, j0:j1], ALU.mult
             )
             if j1 == S:
                 nc.sync.dma_start(out[n * P : (n + 1) * P, :], window[:])
 
-        last = PASSES - 1
-        tab_s = keep.tile([P, T // 4], I32, name="tab_s", align_bytes=64)
+        tab_s = staged([P, T // 4], I32, "tab_s", 6 * SLOT - 1024)
         nc.gpsimd.memset(tab_s[:], 0)
-        tab_w[0] = staged([P, T], I32, "tab_w0", SLOT)
+        tab_w[0] = staged([P, T], I32, "tab_w0", SLOT // 2)
         load_table_columns(0, 0, T // 2)
         nc.sync.dma_start(pick[:], offs)
         for a in range(PASSES):
@@ -223,31 +233,36 @@ def tile_list_shortlist_coding_residual_kernel(
             nc.sync.dma_start(tab_s[row0 : row0 + 46 : 3, :], tab_scales[a].bitcast(I32))
         nc.gpsimd.dma_start(bias[:], benc.rearrange("(p t) -> p t", t=4))
         nc.vector.memset(doc_s[:], 0)
-        cache.append(keep.tile([P, T2], F32, name="cache1"))
-        for window in cache:
-            nc.vector.memset(window[:].bitcast(I32), 0)
+        nc.vector.memset(sk_s[:], 0)
+        cache[0] = kept([P, T2], F32, "cache0")
+        nc.vector.memset(cache[0][:].bitcast(I32), 0)
         load_table_columns(0, T // 2, T)
-        load_enc(0, 0)
+        load_enc(0, 2 * SLOT)
         load_table(1, 3 * SLOT)
-        load_enc(1, 2 * SLOT)
+        load_enc(1, 4 * SLOT)
 
         nc.vector.tensor_copy(doc_s_rows[:], tab_s[:].bitcast(U8).indirect(pick[:]))
+        cache[1] = staged([P, T2], F32, "cache1", 5 * SLOT)
+        nc.gpsimd.memset(cache[1][:], 0.0)
         cast_enc(nc.scalar.copy, 0, 0, P)
         for r in range(4):
             row0 = SCALE_ROW0 + 3 * r
             nc.sync.dma_start(doc_s[r:P:32, :, :], doc_s_rows[row0 : row0 + 45 : 4, :].bitcast(I32))
         nc.sync.dma_start(place[:], offs2)
-        load_enc(last, 0)
+        load_enc(LAST, 6 * SLOT)
+        for a in range(LAST):
+            doc_tile(a, 0, S)
         gather_words(0, 0, S)
-        load_table(last, SLOT)
-        load_dec(0, 128)
-        load_sketch_scales(0, 2)
-        load_sketch(0, 2)
-        load_dec(128, 256)
+        cache[2] = staged([P, T2], F32, "cache2", 0)
+        nc.gpsimd.memset(cache[2][:], 0.0)
+        load_table(LAST, SLOT)
+        load_dec(0, 256)
+        for r in range(4):
+            nc.sync.dma_start(sk_s[r:P:32, :, :], wsk_scales[:, r:16:4, :].bitcast(I32).rearrange("a q n -> q a n"))
+        load_sketch(0, EARLY)
         nc.sync.dma_start(weight[:], wgo)
+        load_sketch(EARLY, ROW_TILES)
         load_dec(256, 512)
-        load_sketch(2, ROW_TILES)
-        load_sketch_scales(2, ROW_TILES)
         load_dec(512, N)
         gather_words(1, 0, 512)
         quant_enc(0)
@@ -255,67 +270,88 @@ def tile_list_shortlist_coding_residual_kernel(
         cast_enc(nc.scalar.copy, 1, 0, 64)
         cast_enc(nc.vector.tensor_copy, 1, 64, P)
         quant_enc(1)
-        cast_enc(nc.scalar.copy, last, 0, 48)
-        cast_enc(nc.vector.tensor_copy, last, 48, P)
-        quant_enc(last)
-        cast_dec(0, 0, 128)
-        quant_dec(0, 128)
+        cast_enc(nc.scalar.copy, LAST, 0, 48)
+        cast_enc(nc.vector.tensor_copy, LAST, 48, P)
+        quant_enc(LAST)
 
-        first = [(bank(0), (0, 1), 0, 256), (bank(1), (2, 3), 0, 256)]
-        second = [(bank(2), (0, 1), 256, 512), (bank(3), (2, 3), 256, 512)]
-        third = [(bank(6), (0,), 512, S), (bank(7), (1,), 512, S)]
-        for a in range(last):
-            for acc, ts, j0, j1 in first + second + third:
+        halves = [(bank(0), (0, 1, 2, 3), 0, 128), (bank(1), (0, 1, 2, 3), 128, 256)]
+        second = [(bank(2), (0, 1), 256, 512)]
+        shared = [(bank(3), 2, 0), (bank(6), 3, 128)]
+        for a in range(LAST):
+            for acc, ts, j0, j1 in halves + second:
                 encode_pass(acc, ts, a, j0, j1)
+            for acc, t, j0 in shared:
+                encode_pass(acc, (t,), a, 256, 512)
 
-        gather_words(last, 0, 256)
-        gather_words(last, 256, 512)
-        gather_words(last, 512, S)
-        for acc, ts, j0, j1 in first:
-            encode_pass(acc, ts, last, j0, j1)
-            relu(acc, ts, j0, j1)
-        interleave(nc.vector.tensor_copy, 0, 256)
-        quant_code(0, 256)
-        residual(4, 0, 0, 256, True, sized(0, 0, 256, "size_a0"))
-        cast_dec(128, 128, 256, True)
-        quant_dec(128, 256)
+        doc_tile(LAST, 0, 256)
+        doc_tile(LAST, 256, 512)
+        gather_words(LAST, 0, 128)
+        gather_words(LAST, 128, 256)
+        gather_words(LAST, 256, 512)
+        for acc, ts, j0, j1 in halves + second:
+            encode_pass(acc, ts, LAST, j0, j1)
+        for acc, t, j0 in shared:
+            encode_pass(acc, (t,), LAST, 256, 512, False)
+        dec_bf[0] = kept([P, 256, 4], BF16, "dec_bf0")[:]
+        cast_dec(0, 256)
+        for acc, ts, j0, j1 in halves:
+            add_bias(acc, j0)
+        for acc, ts, j0, j1 in halves:
+            clip(j0)
+        quant_dec(0, 256)
+        for acc, ts, j0, j1 in halves:
+            quant_code(j0, j1)
         for acc, ts, j0, j1 in second:
-            encode_pass(acc, ts, last, j0, j1)
-            relu(acc, ts, j0, j1)
+            relu(acc, ts, j0)
+        doc_tile(LAST, 512, S, "code_bf0")
+        gather_words(LAST, 512, S)
+        first = sized(0, 0, 256)
+        for acc, t, j0 in shared:
+            residual(acc[:, STRETCH:], 0, j0, j0 + P, first[:, j0 : j0 + P], True, False)
+            relu(acc, (t,), 256)
         scatter(0, 0, 256)
-        interleave(nc.vector.tensor_copy, 256, 512)
+        interleave(256)
         quant_code(256, 512)
-        residual(5, 1, 0, 256, True, sized(1, 0, 256, "size_a1"))
-        for acc, ts, j0, j1 in third:
-            encode_pass(acc, ts, last, j0, j1)
-            relu(acc, ts, j0, j1)
+        residual(bank(7), 1, 0, 256, sized(1, 0, 256, "planes256"))
         scatter(1, 0, 256)
-        for b, t in ((2, 2), (3, 3)):
-            acc = bank(b)
-            for a in range(PASSES):
-                encode_pass(acc, (t,), a, 512, S)
-            relu(acc, (t,), 512, S)
-        interleave(nc.scalar.copy, 512, 768)
-        quant_code(512, 768)
-        residual(0, 0, 256, 512, False, sized(0, 256, 512, "planes512"))
+
+        def encode(banks, j0):
+            for u, b in enumerate(banks):
+                acc, ts = bank(b), (2 * u, 2 * u + 1)
+                for a in range(PASSES):
+                    encode_pass(acc, ts, a, j0, j0 + STRETCH)
+                relu(acc, ts, j0)
+
+        encode((3, 6), 512)
+        residual(bank(4), 0, 256, 512, sized(0, 256, 512))
         scatter(0, 256, 512)
-        interleave(nc.scalar.copy, 768, S)
-        quant_code(768, S)
-        residual(1, 1, 256, 512, False, sized(1, 256, 512, "planes768"))
+        interleave(512)
+        quant_code(512, 768)
+        residual(bank(5), 1, 256, 512, sized(1, 256, 512, "planes512"))
         scatter(1, 256, 512)
-        cache.append(keep.tile([P, T2], F32, name="cache2", tag="planes768", align_bytes=64))
-        nc.gpsimd.memset(cache[2][:], 0.0)
-        cast_dec(256, 256, 512)
+
+        planes[768] = staged([P, 4, STRETCH], BF16, "planes768", 7 * SLOT)
+        encode((7, 4), 768)
+        residual(bank(0), 0, 512, 768, sized(0, 512, 768), False)
+        scatter(0, 512, 768)
+        interleave(768)
+        quant_code(768, S)
+        size[1, 512] = staged([P, STRETCH], F32, "size1_512", 7 * SLOT)
+        residual(bank(1), 1, 512, 768, size[1, 512][:], False)
+        scatter(1, 512, 768)
+
+        rest = staged([P, 512, 4], BF16, "dec_bf_rest", 7 * SLOT + 1024)
+        dec_bf[256], dec_bf[512] = rest[:, 0:256, :], rest[:, 256:512, :]
+        cast_dec(256, 512)
         quant_dec(256, 512)
-        residual(4, 0, 512, S, True, sized(0, 512, S, "dec_raw256"))
-        scatter(0, 512, S)
-        cast_dec(512, 512, N)
+        for n in range(EARLY):
+            residual(bank((3, 6)[n]), n, 768, S, sized(n, 768, S))
+            scatter(n, 768, S)
+        cast_dec(512, N)
         quant_dec(512, N)
-        residual(5, 1, 512, S, True, sized(1, 512, S, "dec_raw512"))
-        scatter(1, 512, S)
-        for n in range(2, ROW_TILES):
-            whole = sized(n, 0, S, "size%d" % n)
+        for n, banks in zip(range(EARLY, ROW_TILES), ((0, 1), (7, 4), (2, 5), (3, 6))):
+            whole = sized(n, 0, S)
             for half in range(2):
                 j0 = 512 * half
-                residual((2 * n + half + 2) % 8, n, j0, j0 + 512, True, whole[:, j0 : j0 + 512])
+                residual(bank(banks[half]), n, j0, j0 + 512, whole[:, j0 : j0 + 512], banks[half] != 2)
             scatter(n, 0, S)

@@ -48,7 +48,7 @@ def tile_list_shortlist_coding_residual_kernel(
         bias = kept([P, 4], F32, "bias")
         weight = kept([P, S], F32, "weight")
         doc_s_rows = kept([P, S], U8, "doc_s_rows")
-        doc_s = kept([P, PASSES, S // 4], I32, "doc_s")
+        doc_s = [kept([P, PASSES, S // 8], I32, "doc_s%d" % h) for h in range(2)]
         enc_bf = [kept([P, 4, P, 4], BF16, "enc_bf%d" % a) for a in range(PASSES)]
         enc_w = [kept([P, H], U32, "enc_w%d" % a) for a in range(PASSES)]
         enc_s = [kept([P, H], U8, "enc_s%d" % a) for a in range(PASSES)]
@@ -56,8 +56,7 @@ def tile_list_shortlist_coding_residual_kernel(
         dec_s = kept([P, N], U8, "dec_s")
         code_w = kept([P, S], U32, "code_w")
         code_s = kept([P, S], U8, "code_s")
-        sk_s = kept([P, PASSES, N // 4], I32, "sk_s")
-        tab_w, enc_raw, dec_raw, dec_bf, sk_w, doc_w, code_bf, planes, size, cache = ({} for i in range(10))
+        tab_w, enc_raw, dec_raw, dec_bf, sk_w, sk_s, doc_w, code_bf, planes, size, cache = ({} for i in range(11))
 
         def load_table_columns(a, t0, t1):
             words = tab_words[a].rearrange("p t i -> p (t i)").bitcast(I32)
@@ -80,6 +79,27 @@ def tile_list_shortlist_coding_residual_kernel(
             nc.sync.dma_start(words[:], wsk_words.bitcast(I32).rearrange("a p c -> p a c")[:, :, 64 * n0 : 64 * n1])
             for n in range(n0, n1):
                 sk_w[n] = words[:, :, 64 * (n - n0) : 64 * (n - n0 + 1)]
+
+        def load_sketch_scales(n0, n1):
+            rows = kept([P, PASSES, 32 * (n1 - n0)], I32, "sk_s%d" % n0)
+            nc.vector.memset(rows[:], 0)
+            for r in range(4):
+                nc.sync.dma_start(
+                    rows[r:P:32, :, :],
+                    wsk_scales[:, r:16:4, :].bitcast(I32).rearrange("a q n -> q a n")[:, :, 32 * n0 : 32 * n1],
+                )
+            for n in range(n0, n1):
+                sk_s[n] = rows[:, :, 32 * (n - n0) : 32 * (n - n0 + 1)]
+
+        def move_doc_scales(h):
+            for r in range(4):
+                row0 = SCALE_ROW0 + 3 * r
+                nc.sync.dma_start(
+                    doc_s[h][r:P:32, :, :], doc_s_rows[row0 : row0 + 45 : 4, 512 * h : 512 * (h + 1)].bitcast(I32)
+                )
+
+        def load_weight(j0, j1):
+            nc.sync.dma_start(weight[:, j0:j1], wgo[:, j0:j1])
 
         def doc_tile(a, j0, j1, tag=None):
             tile = kept([P, j1 - j0], U32, "doc_w%d_%d" % (a, j0), tag)
@@ -122,7 +142,7 @@ def tile_list_shortlist_coding_residual_kernel(
             )
 
         def doc_operand(a, j0, j1):
-            return doc_words(a, j0, j1).bitcast(FP8X4), doc_s[:, a, :].bitcast(U8)[:, j0:j1]
+            return doc_words(a, j0, j1).bitcast(FP8X4), doc_s[j0 // 512][:, a, :].bitcast(U8)[:, j0 % 512 : j0 % 512 + j1 - j0]
 
         def encode_pass(acc, ts, a, j0, j1, closes=True):
             width = j1 - j0
@@ -180,7 +200,7 @@ def tile_list_shortlist_coding_residual_kernel(
                 nc.tensor.matmul_mx(
                     out=acc[:, g0 - j0 : g1 - j0],
                     lhsT=sk_w[n][:, a, :].bitcast(U8).bitcast(FP4X4),
-                    lhsT_scale=sk_s[:, a, :].bitcast(U8)[:, n * P : (n + 1) * P],
+                    lhsT_scale=sk_s[n][:, a, :].bitcast(U8),
                     rhs=rhs,
                     rhs_scale=rhs_scale,
                     start=(start and i == 0),
@@ -232,8 +252,8 @@ def tile_list_shortlist_coding_residual_kernel(
             row0 = SCALE_ROW0 + 4 * a
             nc.sync.dma_start(tab_s[row0 : row0 + 46 : 3, :], tab_scales[a].bitcast(I32))
         nc.gpsimd.dma_start(bias[:], benc.rearrange("(p t) -> p t", t=4))
-        nc.vector.memset(doc_s[:], 0)
-        nc.vector.memset(sk_s[:], 0)
+        for rows in doc_s:
+            nc.vector.memset(rows[:], 0)
         cache[0] = kept([P, T2], F32, "cache0")
         nc.vector.memset(cache[0][:].bitcast(I32), 0)
         load_table_columns(0, T // 2, T)
@@ -245,9 +265,7 @@ def tile_list_shortlist_coding_residual_kernel(
         cache[1] = staged([P, T2], F32, "cache1", 5 * SLOT)
         nc.gpsimd.memset(cache[1][:], 0.0)
         cast_enc(nc.scalar.copy, 0, 0, P)
-        for r in range(4):
-            row0 = SCALE_ROW0 + 3 * r
-            nc.sync.dma_start(doc_s[r:P:32, :, :], doc_s_rows[row0 : row0 + 45 : 4, :].bitcast(I32))
+        move_doc_scales(0)
         nc.sync.dma_start(place[:], offs2)
         load_enc(LAST, 6 * SLOT)
         for a in range(LAST):
@@ -257,12 +275,14 @@ def tile_list_shortlist_coding_residual_kernel(
         nc.gpsimd.memset(cache[2][:], 0.0)
         load_table(LAST, SLOT)
         load_dec(0, 256)
-        for r in range(4):
-            nc.sync.dma_start(sk_s[r:P:32, :, :], wsk_scales[:, r:16:4, :].bitcast(I32).rearrange("a q n -> q a n"))
+        load_sketch_scales(0, EARLY)
         load_sketch(0, EARLY)
-        nc.sync.dma_start(weight[:], wgo)
-        load_sketch(EARLY, ROW_TILES)
+        load_weight(0, 256)
+        move_doc_scales(1)
+        load_weight(256, S)
         load_dec(256, 512)
+        load_sketch(EARLY, ROW_TILES)
+        load_sketch_scales(EARLY, ROW_TILES)
         load_dec(512, N)
         gather_words(1, 0, 512)
         quant_enc(0)

@@ -251,7 +251,7 @@ def tile_list_shortlist_coding_residual_kernel(
         for a in range(PASSES):
             row0 = SCALE_ROW0 + 4 * a
             nc.sync.dma_start(tab_s[row0 : row0 + 46 : 3, :], tab_scales[a].bitcast(I32))
-        nc.gpsimd.dma_start(bias[:], benc.rearrange("(p t) -> p t", t=4))
+        nc.scalar.dma_start(bias[:], benc.rearrange("(p t) -> p t", t=4))
         for rows in doc_s:
             nc.vector.memset(rows[:], 0)
         cache[0] = kept([P, T2], F32, "cache0")
@@ -271,8 +271,6 @@ def tile_list_shortlist_coding_residual_kernel(
         for a in range(LAST):
             doc_tile(a, 0, S)
         gather_words(0, 0, S)
-        cache[2] = staged([P, T2], F32, "cache2", 0)
-        nc.gpsimd.memset(cache[2][:], 0.0)
         load_table(LAST, SLOT)
         load_dec(0, 256)
         load_sketch_scales(0, EARLY)
@@ -347,6 +345,8 @@ def tile_list_shortlist_coding_residual_kernel(
         scatter(0, 256, 512)
         interleave(512)
         quant_code(512, 768)
+        cache[2] = kept([P, T2], F32, "cache2", "code_bf512")
+        nc.gpsimd.memset(cache[2][:], 0.0)
         residual(bank(5), 1, 256, 512, sized(1, 256, 512, "planes512"))
         scatter(1, 256, 512)
 

@@ -261,7 +261,10 @@ def tile_list_shortlist_coding_residual_kernel(
         load_table(1, 3 * SLOT)
         load_enc(1, 4 * SLOT)
 
-        nc.vector.tensor_copy(doc_s_rows[:], tab_s[:].bitcast(U8).indirect(pick[:]))
+        for j0 in (0, 512):
+            nc.vector.tensor_copy(
+                doc_s_rows[:, j0 : j0 + 512], tab_s[:].bitcast(U8).indirect(pick[:, j0 // 16 : j0 // 16 + 32])
+            )
         cache[1] = staged([P, T2], F32, "cache1", 5 * SLOT)
         nc.gpsimd.memset(cache[1][:], 0.0)
         cast_enc(nc.scalar.copy, 0, 0, P)
@@ -288,8 +291,8 @@ def tile_list_shortlist_coding_residual_kernel(
         cast_enc(nc.scalar.copy, 1, 0, 64)
         cast_enc(nc.vector.tensor_copy, 1, 64, P)
         quant_enc(1)
-        cast_enc(nc.scalar.copy, LAST, 0, 48)
-        cast_enc(nc.vector.tensor_copy, LAST, 48, P)
+        cast_enc(nc.scalar.copy, LAST, 0, 40)
+        cast_enc(nc.vector.tensor_copy, LAST, 40, P)
         quant_enc(LAST)
 
         halves = [(bank(0), (0, 1, 2, 3), 0, 128), (bank(1), (0, 1, 2, 3), 128, 256)]

@@ -296,13 +296,12 @@ def tile_list_shortlist_coding_residual_kernel(
         quant_enc(LAST)
 
         halves = [(bank(0), (0, 1, 2, 3), 0, 128), (bank(1), (0, 1, 2, 3), 128, 256)]
-        second = [(bank(2), (0, 1), 256, 512)]
-        shared = [(bank(3), 2, 0), (bank(6), 3, 128)]
+        second = [(bank(2), (0, 1), 256, 512), (bank(6), (2,), 256, 512)]
+        shared = bank(3)
         for a in range(LAST):
             for acc, ts, j0, j1 in halves + second:
                 encode_pass(acc, ts, a, j0, j1)
-            for acc, t, j0 in shared:
-                encode_pass(acc, (t,), a, 256, 512)
+            encode_pass(shared, (3,), a, 256, 512)
 
         doc_tile(LAST, 0, 256)
         doc_tile(LAST, 256, 512)
@@ -311,8 +310,7 @@ def tile_list_shortlist_coding_residual_kernel(
         gather_words(LAST, 256, 512)
         for acc, ts, j0, j1 in halves + second:
             encode_pass(acc, ts, LAST, j0, j1)
-        for acc, t, j0 in shared:
-            encode_pass(acc, (t,), LAST, 256, 512, False)
+        encode_pass(shared, (3,), LAST, 256, 512, False)
         dec_bf[0] = kept([P, 256, 4], BF16, "dec_bf0")[:]
         cast_dec(0, 256)
         for acc, ts, j0, j1 in halves:
@@ -327,9 +325,9 @@ def tile_list_shortlist_coding_residual_kernel(
         doc_tile(LAST, 512, S, "code_bf0")
         gather_words(LAST, 512, S)
         first = sized(0, 0, 256)
-        for acc, t, j0 in shared:
-            residual(acc[:, STRETCH:], 0, j0, j0 + P, first[:, j0 : j0 + P], True, False)
-            relu(acc, (t,), 256)
+        residual(bank(7), 0, 0, P, first[:, 0:P])
+        residual(shared[:, STRETCH:], 0, P, 256, first[:, P:256], True, False)
+        relu(shared, (3,), 256)
         scatter(0, 0, 256)
         interleave(256)
         quant_code(256, 512)
@@ -343,7 +341,7 @@ def tile_list_shortlist_coding_residual_kernel(
                     encode_pass(acc, ts, a, j0, j0 + STRETCH)
                 relu(acc, ts, j0)
 
-        encode((3, 6), 512)
+        encode((6, 3), 512)
         residual(bank(4), 0, 256, 512, sized(0, 256, 512))
         scatter(0, 256, 512)
         interleave(512)

@@ -91,6 +91,22 @@ def tile_list_shortlist_coding_residual_kernel(
             for n in range(n0, n1):
                 sk_s[n] = rows[:, :, 32 * (n - n0) : 32 * (n - n0 + 1)]
 
+        def load_early_sketch_scales():
+            width = 32 * EARLY
+            rows = staged([4, PASSES, 4, width], I32, "sk_s_rows", 8 * SLOT)
+            src = wsk_scales.bitcast(I32).rearrange("a (g r) n -> r (a g) n", g=4)
+            nc.scalar.dma_start(rows[:].rearrange("p a g n -> p (a g) n"), src[:, :, 0:width])
+            return rows
+
+        def lift_early_sketch_scales(rows):
+            width = 32 * EARLY
+            lifted = kept([P, PASSES, width], I32, "sk_s_early")
+            nc.vector.memset(lifted[:], 0)
+            for g in range(4):
+                nc.vector.tensor_copy(lifted[32 * g : 32 * g + 4, :, :], rows[:, :, g, :])
+            for n in range(EARLY):
+                sk_s[n] = lifted[:, :, 32 * n : 32 * (n + 1)]
+
         def move_doc_scales(h):
             for r in range(4):
                 row0 = SCALE_ROW0 + 3 * r
@@ -101,8 +117,9 @@ def tile_list_shortlist_coding_residual_kernel(
         def load_weight(j0, j1):
             nc.sync.dma_start(weight[:, j0:j1], wgo[:, j0:j1])
 
-        def doc_tile(a, j0, j1, tag=None):
-            tile = kept([P, j1 - j0], U32, "doc_w%d_%d" % (a, j0), tag)
+        def doc_tile(a, j0, j1, offset=None):
+            name = "doc_w%d_%d" % (a, j0)
+            tile = kept([P, j1 - j0], U32, name) if offset is None else staged([P, j1 - j0], U32, name, offset)
             for g in range(j0, j1, P):
                 doc_w[a, g] = (tile, j0)
 
@@ -134,6 +151,11 @@ def tile_list_shortlist_coding_residual_kernel(
                 scale=-1.0,
             )
 
+        def cast_dec_gpsimd(c0, c1):
+            nc.gpsimd.tensor_scalar(
+                dec_bf[c0], dec_raw[c0][:].rearrange("p j c -> p c j"), -1.0, 0.0, ALU.mult, ALU.add
+            )
+
         def quant_dec(c0, c1):
             nc.vector.quantize_mx(
                 out=dec_w[:, c0:c1].bitcast(FP8X4),
@@ -144,7 +166,7 @@ def tile_list_shortlist_coding_residual_kernel(
         def doc_operand(a, j0, j1):
             return doc_words(a, j0, j1).bitcast(FP8X4), doc_s[j0 // 512][:, a, :].bitcast(U8)[:, j0 % 512 : j0 % 512 + j1 - j0]
 
-        def encode_pass(acc, ts, a, j0, j1, closes=True):
+        def encode_pass(acc, ts, a, j0, j1, closes=True, first=0, last=LAST):
             width = j1 - j0
             rhs, rhs_scale = doc_operand(a, j0, j1)
             for u, t in enumerate(ts):
@@ -154,8 +176,8 @@ def tile_list_shortlist_coding_residual_kernel(
                     lhsT_scale=enc_s[a][:, t * P : (t + 1) * P],
                     rhs=rhs,
                     rhs_scale=rhs_scale,
-                    start=(a == 0 and u == 0),
-                    stop=(closes and a == LAST and u == len(ts) - 1),
+                    start=(a == first and u == 0),
+                    stop=(closes and a == last and u == len(ts) - 1),
                 )
 
         def add_bias(acc, j0):
@@ -171,17 +193,18 @@ def tile_list_shortlist_coding_residual_kernel(
             flat = code_bf[j0][:].rearrange("p c t -> p (c t)")
             nc.vector.tensor_scalar(flat, flat, 0.0, None, ALU.max)
 
-        def relu(acc, ts, j0):
+        def relu(acc, ts, j0, width=STRETCH):
             if j0 not in planes:
-                planes[j0] = kept([P, 4, STRETCH], BF16, "planes%d" % j0)
+                planes[j0] = kept([P, 4, width], BF16, "planes%d" % j0)
             for u, t in enumerate(ts):
                 nc.scalar.activation(
-                    planes[j0][:, t, :], acc[:, u * STRETCH : (u + 1) * STRETCH], ACT.Relu, bias=bias[:, t : t + 1]
+                    planes[j0][:, t, :], acc[:, u * width : (u + 1) * width], ACT.Relu, bias=bias[:, t : t + 1]
                 )
 
-        def interleave(j0):
-            code_bf[j0] = kept([P, STRETCH, 4], BF16, "code_bf%d" % j0)
-            nc.scalar.copy(
+        def interleave(j0, engine_copy=nc.scalar.copy, width=STRETCH):
+            if j0 not in code_bf:
+                code_bf[j0] = kept([P, width, 4], BF16, "code_bf%d" % j0)
+            engine_copy(
                 code_bf[j0][:].rearrange("p (c i) t -> p c t i", i=4),
                 planes[j0][:].rearrange("p t (c i) -> p c t i", i=4),
             )
@@ -252,10 +275,12 @@ def tile_list_shortlist_coding_residual_kernel(
             row0 = SCALE_ROW0 + 4 * a
             nc.sync.dma_start(tab_s[row0 : row0 + 46 : 3, :], tab_scales[a].bitcast(I32))
         nc.scalar.dma_start(bias[:], benc.rearrange("(p t) -> p t", t=4))
+        early_rows = load_early_sketch_scales()
         for rows in doc_s:
             nc.vector.memset(rows[:], 0)
-        cache[0] = kept([P, T2], F32, "cache0")
-        nc.vector.memset(cache[0][:].bitcast(I32), 0)
+        lift_early_sketch_scales(early_rows)
+        cache[0] = staged([P, T2], F32, "cache0", 8 * SLOT)
+        nc.gpsimd.memset(cache[0][:], 0.0)
         load_table_columns(0, T // 2, T)
         load_enc(0, 2 * SLOT)
         load_table(1, 3 * SLOT)
@@ -275,9 +300,9 @@ def tile_list_shortlist_coding_residual_kernel(
             doc_tile(a, 0, S)
         gather_words(0, 0, S)
         load_table(LAST, SLOT)
-        load_dec(0, 256)
-        load_sketch_scales(0, EARLY)
+        load_dec(0, P)
         load_sketch(0, EARLY)
+        load_dec(P, 256)
         load_weight(0, 256)
         move_doc_scales(1)
         load_weight(256, S)
@@ -311,18 +336,22 @@ def tile_list_shortlist_coding_residual_kernel(
         for acc, ts, j0, j1 in halves + second:
             encode_pass(acc, ts, LAST, j0, j1)
         encode_pass(shared, (3,), LAST, 256, 512, False)
-        dec_bf[0] = kept([P, 256, 4], BF16, "dec_bf0")[:]
-        cast_dec(0, 256)
-        for acc, ts, j0, j1 in halves:
-            add_bias(acc, j0)
-        for acc, ts, j0, j1 in halves:
-            clip(j0)
-        quant_dec(0, 256)
+        dec_bf[0] = staged([P, P, 4], BF16, "dec_bf0", 0)[:]
+        code_bf[0] = staged([P, P, 4], BF16, "code_bf0", 1024)
+        dec_bf[P] = kept([P, P, 4], BF16, "dec_bf128")[:]
+        cast_dec_gpsimd(0, P)
+        relu(halves[0][0], (0, 1, 2, 3), 0, P)
+        add_bias(halves[1][0], P)
+        interleave(0, nc.vector.tensor_copy, P)
+        clip(P)
+        quant_dec(0, P)
         for acc, ts, j0, j1 in halves:
             quant_code(j0, j1)
+        cast_dec(P, 256)
+        quant_dec(P, 256)
         for acc, ts, j0, j1 in second:
             relu(acc, ts, j0)
-        doc_tile(LAST, 512, S, "code_bf0")
+        doc_tile(LAST, 512, S, 0)
         gather_words(LAST, 512, S)
         first = sized(0, 0, 256)
         residual(bank(7), 0, 0, P, first[:, 0:P])
@@ -331,34 +360,34 @@ def tile_list_shortlist_coding_residual_kernel(
         scatter(0, 0, 256)
         interleave(256)
         quant_code(256, 512)
-        residual(bank(7), 1, 0, 256, sized(1, 0, 256, "planes256"))
+        residual(bank(4), 1, 0, 256, sized(1, 0, 256, "planes256"))
         scatter(1, 0, 256)
 
         def encode(banks, j0):
             for u, b in enumerate(banks):
                 acc, ts = bank(b), (2 * u, 2 * u + 1)
-                for a in range(PASSES):
-                    encode_pass(acc, ts, a, j0, j0 + STRETCH)
+                for a in (LAST, 0, 1):
+                    encode_pass(acc, ts, a, j0, j0 + STRETCH, True, LAST, 1)
                 relu(acc, ts, j0)
 
-        encode((6, 3), 512)
-        residual(bank(4), 0, 256, 512, sized(0, 256, 512))
+        encode((7, 3), 512)
+        residual(bank(2), 0, 256, 512, sized(0, 256, 512))
         scatter(0, 256, 512)
         interleave(512)
         quant_code(512, 768)
         cache[2] = kept([P, T2], F32, "cache2", "code_bf512")
         nc.gpsimd.memset(cache[2][:], 0.0)
-        residual(bank(5), 1, 256, 512, sized(1, 256, 512, "planes512"))
+        residual(bank(6), 1, 256, 512, sized(1, 256, 512, "planes512"))
         scatter(1, 256, 512)
 
         planes[768] = staged([P, 4, STRETCH], BF16, "planes768", 7 * SLOT)
-        encode((7, 4), 768)
-        residual(bank(0), 0, 512, 768, sized(0, 512, 768), False)
+        encode((4, 2), 768)
+        residual(bank(6), 0, 512, 768, sized(0, 512, 768))
         scatter(0, 512, 768)
         interleave(768)
         quant_code(768, S)
         size[1, 512] = staged([P, STRETCH], F32, "size1_512", 7 * SLOT)
-        residual(bank(1), 1, 512, 768, size[1, 512][:], False)
+        residual(bank(7), 1, 512, 768, size[1, 512][:])
         scatter(1, 512, 768)
 
         rest = staged([P, 512, 4], BF16, "dec_bf_rest", 7 * SLOT + 1024)
@@ -366,13 +395,13 @@ def tile_list_shortlist_coding_residual_kernel(
         cast_dec(256, 512)
         quant_dec(256, 512)
         for n in range(EARLY):
-            residual(bank((3, 6)[n]), n, 768, S, sized(n, 768, S))
+            residual(bank((3, 4)[n]), n, 768, S, sized(n, 768, S))
             scatter(n, 768, S)
         cast_dec(512, N)
         quant_dec(512, N)
-        for n, banks in zip(range(EARLY, ROW_TILES), ((0, 1), (7, 4), (2, 5), (3, 6))):
+        for n, banks in zip(range(EARLY, ROW_TILES), ((6, 7), (2, 3), (0, 1), (4, 5))):
             whole = sized(n, 0, S)
             for half in range(2):
                 j0 = 512 * half
-                residual(bank(banks[half]), n, j0, j0 + 512, whole[:, j0 : j0 + 512], banks[half] != 2)
+                residual(bank(banks[half]), n, j0, j0 + 512, whole[:, j0 : j0 + 512], banks[half] not in (0, 1, 5))
             scatter(n, 0, S)

@@ -71,8 +71,10 @@ def tile_list_shortlist_coding_residual_kernel(
             nc.sync.dma_start(enc_raw[a][:], wenc[512 * a : 512 * (a + 1), :].rearrange("(p j) c -> p j c", j=4))
 
         def load_dec(c0, c1):
-            dec_raw[c0] = kept([P, 4, c1 - c0], F32, "dec_raw%d" % c0)
-            nc.sync.dma_start(dec_raw[c0][:], wdec.rearrange("(p j) n -> p j n", j=4)[:, :, c0:c1])
+            raw = kept([P, 4, c1 - c0], F32, "dec_raw%d" % c0)
+            nc.sync.dma_start(raw[:], wdec.rearrange("(p j) n -> p j n", j=4)[:, :, c0:c1])
+            for c in range(c0, c1, P):
+                dec_raw[c] = raw[:, :, c - c0 :]
 
         def load_sketch(n0, n1):
             words = kept([P, PASSES, 64 * (n1 - n0)], I32, "sk_w%d" % n0)
@@ -90,22 +92,6 @@ def tile_list_shortlist_coding_residual_kernel(
                 )
             for n in range(n0, n1):
                 sk_s[n] = rows[:, :, 32 * (n - n0) : 32 * (n - n0 + 1)]
-
-        def load_early_sketch_scales():
-            width = 32 * EARLY
-            rows = staged([4, PASSES, 4, width], I32, "sk_s_rows", 8 * SLOT)
-            src = wsk_scales.bitcast(I32).rearrange("a (g r) n -> r (a g) n", g=4)
-            nc.scalar.dma_start(rows[:].rearrange("p a g n -> p (a g) n"), src[:, :, 0:width])
-            return rows
-
-        def lift_early_sketch_scales(rows):
-            width = 32 * EARLY
-            lifted = kept([P, PASSES, width], I32, "sk_s_early")
-            nc.vector.memset(lifted[:], 0)
-            for g in range(4):
-                nc.vector.tensor_copy(lifted[32 * g : 32 * g + 4, :, :], rows[:, :, g, :])
-            for n in range(EARLY):
-                sk_s[n] = lifted[:, :, 32 * n : 32 * (n + 1)]
 
         def move_doc_scales(h):
             for r in range(4):
@@ -146,14 +132,14 @@ def tile_list_shortlist_coding_residual_kernel(
         def cast_dec(c0, c1):
             nc.scalar.activation(
                 dec_bf[c0].rearrange("p (c i) j -> p c j i", i=4),
-                dec_raw[c0][:].rearrange("p j (c i) -> p c j i", i=4),
+                dec_raw[c0][:, :, 0 : c1 - c0].rearrange("p j (c i) -> p c j i", i=4),
                 ACT.Copy,
                 scale=-1.0,
             )
 
         def cast_dec_gpsimd(c0, c1):
             nc.gpsimd.tensor_scalar(
-                dec_bf[c0], dec_raw[c0][:].rearrange("p j c -> p c j"), -1.0, 0.0, ALU.mult, ALU.add
+                dec_bf[c0], dec_raw[c0][:, :, 0 : c1 - c0].rearrange("p j c -> p c j"), -1.0, 0.0, ALU.mult, ALU.add
             )
 
         def quant_dec(c0, c1):
@@ -275,12 +261,10 @@ def tile_list_shortlist_coding_residual_kernel(
             row0 = SCALE_ROW0 + 4 * a
             nc.sync.dma_start(tab_s[row0 : row0 + 46 : 3, :], tab_scales[a].bitcast(I32))
         nc.scalar.dma_start(bias[:], benc.rearrange("(p t) -> p t", t=4))
-        early_rows = load_early_sketch_scales()
         for rows in doc_s:
             nc.vector.memset(rows[:], 0)
-        lift_early_sketch_scales(early_rows)
-        cache[0] = staged([P, T2], F32, "cache0", 8 * SLOT)
-        nc.gpsimd.memset(cache[0][:], 0.0)
+        cache[0] = kept([P, T2], F32, "cache0")
+        nc.vector.memset(cache[0][:].bitcast(I32), 0)
         load_table_columns(0, T // 2, T)
         load_enc(0, 2 * SLOT)
         load_table(1, 3 * SLOT)
@@ -300,9 +284,9 @@ def tile_list_shortlist_coding_residual_kernel(
             doc_tile(a, 0, S)
         gather_words(0, 0, S)
         load_table(LAST, SLOT)
-        load_dec(0, P)
+        load_dec(0, 256)
+        load_sketch_scales(0, EARLY)
         load_sketch(0, EARLY)
-        load_dec(P, 256)
         load_weight(0, 256)
         move_doc_scales(1)
         load_weight(256, S)

@@ -93,8 +93,8 @@ def tile_list_shortlist_coding_residual_kernel(
             for n in range(n0, n1):
                 sk_s[n] = rows[:, :, 32 * (n - n0) : 32 * (n - n0 + 1)]
 
-        def move_doc_scales(h):
-            for r in range(4):
+        def move_doc_scales(h, r0=0, r1=4):
+            for r in range(r0, r1):
                 row0 = SCALE_ROW0 + 3 * r
                 nc.sync.dma_start(
                     doc_s[h][r:P:32, :, :], doc_s_rows[row0 : row0 + 45 : 4, 512 * h : 512 * (h + 1)].bitcast(I32)
@@ -169,9 +169,9 @@ def tile_list_shortlist_coding_residual_kernel(
         def add_bias(acc, j0):
             code_bf[j0] = kept([P, P, 4], BF16, "code_bf%d" % j0)
             nc.vector.tensor_tensor(
-                code_bf[j0][:],
-                acc[:].rearrange("p (t c) -> p c t", t=4),
-                bias[:].unsqueeze(1).to_broadcast([P, P, 4]),
+                code_bf[j0][:].rearrange("p (c i) t -> p c t i", i=2),
+                acc[:].rearrange("p (t c i) -> p c t i", t=4, i=2),
+                bias[:].unsqueeze(1).unsqueeze(3).to_broadcast([P, P // 2, 4, 2]),
                 ALU.add,
             )
 
@@ -287,8 +287,9 @@ def tile_list_shortlist_coding_residual_kernel(
         load_dec(0, 256)
         load_sketch_scales(0, EARLY)
         load_sketch(0, EARLY)
+        move_doc_scales(1, 0, 3)
         load_weight(0, 256)
-        move_doc_scales(1)
+        move_doc_scales(1, 3, 4)
         load_weight(256, S)
         load_dec(256, 512)
         load_sketch(EARLY, ROW_TILES)
@@ -317,6 +318,8 @@ def tile_list_shortlist_coding_residual_kernel(
         gather_words(LAST, 0, 128)
         gather_words(LAST, 128, 256)
         gather_words(LAST, 256, 512)
+        doc_tile(LAST, 512, 768)
+        gather_words(LAST, 512, 768)
         for acc, ts, j0, j1 in halves + second:
             encode_pass(acc, ts, LAST, j0, j1)
         encode_pass(shared, (3,), LAST, 256, 512, False)
@@ -335,8 +338,8 @@ def tile_list_shortlist_coding_residual_kernel(
         quant_dec(P, 256)
         for acc, ts, j0, j1 in second:
             relu(acc, ts, j0)
-        doc_tile(LAST, 512, S, 0)
-        gather_words(LAST, 512, S)
+        doc_tile(LAST, 768, S, 512)
+        gather_words(LAST, 768, S)
         first = sized(0, 0, 256)
         residual(bank(7), 0, 0, P, first[:, 0:P])
         residual(shared[:, STRETCH:], 0, P, 256, first[:, P:256], True, False)

@@ -358,18 +358,18 @@ def tile_list_shortlist_coding_residual_kernel(
                 relu(acc, ts, j0)
 
         encode((7, 3), 512)
-        residual(bank(2), 0, 256, 512, sized(0, 256, 512))
+        residual(bank(4), 0, 256, 512, sized(0, 256, 512))
         scatter(0, 256, 512)
         interleave(512)
         quant_code(512, 768)
         cache[2] = kept([P, T2], F32, "cache2", "code_bf512")
         nc.gpsimd.memset(cache[2][:], 0.0)
-        residual(bank(6), 1, 256, 512, sized(1, 256, 512, "planes512"))
+        residual(bank(4), 1, 256, 512, sized(1, 256, 512, "planes512"))
         scatter(1, 256, 512)
 
         planes[768] = staged([P, 4, STRETCH], BF16, "planes768", 7 * SLOT)
-        encode((4, 2), 768)
-        residual(bank(6), 0, 512, 768, sized(0, 512, 768))
+        encode((7, 3), 768)
+        residual(bank(4), 0, 512, 768, sized(0, 512, 768))
         scatter(0, 512, 768)
         interleave(768)
         quant_code(768, S)
@@ -386,9 +386,9 @@ def tile_list_shortlist_coding_residual_kernel(
             scatter(n, 768, S)
         cast_dec(512, N)
         quant_dec(512, N)
-        for n, banks in zip(range(EARLY, ROW_TILES), ((6, 7), (2, 3), (0, 1), (4, 5))):
+        for n, banks in zip(range(EARLY, ROW_TILES), ((7, 3), (4, 0), (2, 1), (6, 5))):
             whole = sized(n, 0, S)
             for half in range(2):
                 j0 = 512 * half
-                residual(bank(banks[half]), n, j0, j0 + 512, whole[:, j0 : j0 + 512], banks[half] not in (0, 1, 5))
+                residual(bank(banks[half]), n, j0, j0 + 512, whole[:, j0 : j0 + 512], banks[half] in (3, 4, 7))
             scatter(n, 0, S)

@@ -318,8 +318,6 @@ def tile_list_shortlist_coding_residual_kernel(
         gather_words(LAST, 0, 128)
         gather_words(LAST, 128, 256)
         gather_words(LAST, 256, 512)
-        doc_tile(LAST, 512, 768)
-        gather_words(LAST, 512, 768)
         for acc, ts, j0, j1 in halves + second:
             encode_pass(acc, ts, LAST, j0, j1)
         encode_pass(shared, (3,), LAST, 256, 512, False)
@@ -338,8 +336,8 @@ def tile_list_shortlist_coding_residual_kernel(
         quant_dec(P, 256)
         for acc, ts, j0, j1 in second:
             relu(acc, ts, j0)
-        doc_tile(LAST, 768, S, 512)
-        gather_words(LAST, 768, S)
+        doc_tile(LAST, 512, S, 0)
+        gather_words(LAST, 512, S)
         first = sized(0, 0, 256)
         residual(bank(7), 0, 0, P, first[:, 0:P])
         residual(shared[:, STRETCH:], 0, P, 256, first[:, P:256], True, False)
@@ -357,8 +355,8 @@ def tile_list_shortlist_coding_residual_kernel(
                     encode_pass(acc, ts, a, j0, j0 + STRETCH, True, LAST, 1)
                 relu(acc, ts, j0)
 
-        encode((7, 3), 512)
-        residual(bank(4), 0, 256, 512, sized(0, 256, 512))
+        encode((0, 3), 512)
+        residual(bank(7), 0, 256, 512, sized(0, 256, 512))
         scatter(0, 256, 512)
         interleave(512)
         quant_code(512, 768)
@@ -368,13 +366,13 @@ def tile_list_shortlist_coding_residual_kernel(
         scatter(1, 256, 512)
 
         planes[768] = staged([P, 4, STRETCH], BF16, "planes768", 7 * SLOT)
-        encode((7, 3), 768)
+        encode((0, 7), 768)
         residual(bank(4), 0, 512, 768, sized(0, 512, 768))
         scatter(0, 512, 768)
         interleave(768)
         quant_code(768, S)
         size[1, 512] = staged([P, STRETCH], F32, "size1_512", 7 * SLOT)
-        residual(bank(7), 1, 512, 768, size[1, 512][:])
+        residual(bank(3), 1, 512, 768, size[1, 512][:])
         scatter(1, 512, 768)
 
         rest = staged([P, 512, 4], BF16, "dec_bf_rest", 7 * SLOT + 1024)
@@ -382,13 +380,13 @@ def tile_list_shortlist_coding_residual_kernel(
         cast_dec(256, 512)
         quant_dec(256, 512)
         for n in range(EARLY):
-            residual(bank((3, 4)[n]), n, 768, S, sized(n, 768, S))
+            residual(bank((0, 7)[n]), n, 768, S, sized(n, 768, S))
             scatter(n, 768, S)
         cast_dec(512, N)
         quant_dec(512, N)
-        for n, banks in zip(range(EARLY, ROW_TILES), ((7, 3), (4, 0), (2, 1), (6, 5))):
+        for n, banks in zip(range(EARLY, ROW_TILES), ((4, 3), (0, 7), (2, 1), (6, 5))):
             whole = sized(n, 0, S)
             for half in range(2):
                 j0 = 512 * half
-                residual(bank(banks[half]), n, j0, j0 + 512, whole[:, j0 : j0 + 512], banks[half] in (3, 4, 7))
+                residual(bank(banks[half]), n, j0, j0 + 512, whole[:, j0 : j0 + 512], n < 4)
             scatter(n, 0, S)

from contextlib import ExitStack

import concourse.mybir as mybir

K, H, N, T, S, T2, P = 1536, 512, 768, 2048, 1024, 2048, 128
FLOPS = 2 * S * (K * H + H * N + K * N)

F32 = mybir.dt.float32
BF16 = mybir.dt.bfloat16
I32 = mybir.dt.int32
U32 = mybir.dt.uint32
U16 = mybir.dt.uint16
U8 = mybir.dt.uint8
FP8X4 = mybir.dt.float8_e4m3fn_x4
FP4X4 = mybir.dt.float4_e2m1fn_x4
ACT = mybir.ActivationFunctionType
ALU = mybir.AluOpType

PASSES = K // 512
LAST = PASSES - 1
ROW_TILES = N // P
EARLY = 2
STRETCH = 256
SLOT = 8192
SCALE_ROW0 = 36


def tile_list_shortlist_coding_residual_kernel(
    tc, tab_words, tab_scales, offs, wenc, benc, wdec, wsk_words, wsk_scales, wgo, offs2, out
):
    nc = tc.nc
    with ExitStack() as ctx:
        keep = ctx.enter_context(tc.tile_pool(name="keep", bufs=1))
        stage = ctx.enter_context(tc.tile_pool(name="stage", bufs=1))
        psum = ctx.enter_context(tc.psum_pool(name="psum", bufs=1))

        def kept(shape, dtype, name, tag=None):
            return keep.tile(shape, dtype, name=name, tag=tag or name, align_bytes=64)

        def staged(shape, dtype, name, offset):
            return stage.tile(shape, dtype, name=name, offset=offset, align_bytes=64)

        def bank(b):
            return psum.tile([P, 512], F32, name="bank%d" % b, tag="bank%d" % b)

        pick = keep.tile([P, S // 16], U16, name="pick")
        place = keep.tile([P, S // 16], U16, name="place")
        bias = kept([P, 4], F32, "bias")
        weight = kept([P, S], F32, "weight")
        doc_s_rows = kept([P, S], U8, "doc_s_rows")
        doc_s = [kept([P, PASSES, S // 8], I32, "doc_s%d" % h) for h in range(2)]
        enc_bf = [kept([P, 4, P, 4], BF16, "enc_bf%d" % a) for a in range(PASSES)]
        enc_w = [kept([P, H], U32, "enc_w%d" % a) for a in range(PASSES)]
        enc_s = [kept([P, H], U8, "enc_s%d" % a) for a in range(PASSES)]
        dec_w = kept([P, N], U32, "dec_w")
        dec_s = kept([P, N], U8, "dec_s")
        code_w = kept([P, S], U32, "code_w")
        code_s = kept([P, S], U8, "code_s")
        tab_w, enc_raw, dec_raw, dec_bf, sk_w, sk_s, doc_w, code_bf, planes, size, cache = ({} for i in range(11))

        def load_table_columns(a, t0, t1):
            words = tab_words[a].rearrange("p t i -> p (t i)").bitcast(I32)
            nc.sync.dma_start(tab_w[a][:, t0:t1], words[:, t0:t1])

        def load_table(a, offset):
            tab_w[a] = staged([P, T], I32, "tab_w%d" % a, offset)
            load_table_columns(a, 0, T)

        def load_enc(a, offset):
            enc_raw[a] = staged([P, 4, H], F32, "enc_raw%d" % a, offset)
            nc.sync.dma_start(enc_raw[a][:], wenc[512 * a : 512 * (a + 1), :].rearrange("(p j) c -> p j c", j=4))

        def load_dec(c0, c1):
            raw = kept([P, 4, c1 - c0], F32, "dec_raw%d" % c0)
            nc.sync.dma_start(raw[:], wdec.rearrange("(p j) n -> p j n", j=4)[:, :, c0:c1])
            for c in range(c0, c1, P):
                dec_raw[c] = raw[:, :, c - c0 :]

        def load_sketch(n0, n1):
            words = kept([P, PASSES, 64 * (n1 - n0)], I32, "sk_w%d" % n0)
            nc.sync.dma_start(words[:], wsk_words.bitcast(I32).rearrange("a p c -> p a c")[:, :, 64 * n0 : 64 * n1])
            for n in range(n0, n1):
                sk_w[n] = words[:, :, 64 * (n - n0) : 64 * (n - n0 + 1)]

        def load_sketch_scales(n0, n1):
            rows = kept([P, PASSES, 32 * (n1 - n0)], I32, "sk_s%d" % n0)
            nc.vector.memset(rows[:], 0)
            for r in range(4):
                nc.sync.dma_start(
                    rows[r:P:32, :, :],
                    wsk_scales[:, r:16:4, :].bitcast(I32).rearrange("a q n -> q a n")[:, :, 32 * n0 : 32 * n1],
                )
            for n in range(n0, n1):
                sk_s[n] = rows[:, :, 32 * (n - n0) : 32 * (n - n0 + 1)]

        def move_doc_scales(h, r0=0, r1=4):
            for r in range(r0, r1):
                row0 = SCALE_ROW0 + 3 * r
                nc.sync.dma_start(
                    doc_s[h][r:P:32, :, :], doc_s_rows[row0 : row0 + 45 : 4, 512 * h : 512 * (h + 1)].bitcast(I32)
                )

        def load_weight(j0, j1):
            nc.sync.dma_start(weight[:, j0:j1], wgo[:, j0:j1])

        def doc_tile(a, j0, j1, offset=None):
            name = "doc_w%d_%d" % (a, j0)
            tile = kept([P, j1 - j0], U32, name) if offset is None else staged([P, j1 - j0], U32, name, offset)
            for g in range(j0, j1, P):
                doc_w[a, g] = (tile, j0)

        def doc_words(a, j0, j1):
            tile, first = doc_w[a, j0]
            return tile[:, j0 - first : j1 - first]

        def gather_words(a, j0, j1):
            nc.vector.tensor_copy(doc_words(a, j0, j1), tab_w[a][:].bitcast(U32).indirect(pick[:, j0 // 16 : j1 // 16]))

        def cast_enc(engine_copy, a, m0, m1):
            engine_copy(
                enc_bf[a][:, :, m0:m1, :].rearrange("p t m j -> p m j t"),
                enc_raw[a][:, :, 4 * m0 : 4 * m1].rearrange("p j (m t) -> p m j t", t=4),
            )

        def quant_enc(a):
            nc.vector.quantize_mx(
                out=enc_w[a][:].bitcast(FP8X4),
                scales=enc_s[a][:],
                in_=enc_bf[a][:].rearrange("p t m j -> p (t m j)"),
            )

        def cast_dec(c0, c1):
            nc.scalar.activation(
                dec_bf[c0].rearrange("p (c i) j -> p c j i", i=4),
                dec_raw[c0][:, :, 0 : c1 - c0].rearrange("p j (c i) -> p c j i", i=4),
                ACT.Copy,
                scale=-1.0,
            )

        def cast_dec_gpsimd(c0, c1):
            nc.gpsimd.tensor_scalar(
                dec_bf[c0], dec_raw[c0][:, :, 0 : c1 - c0].rearrange("p j c -> p c j"), -1.0, 0.0, ALU.mult, ALU.add
            )

        def quant_dec(c0, c1):
            nc.vector.quantize_mx(
                out=dec_w[:, c0:c1].bitcast(FP8X4),
                scales=dec_s[:, c0:c1],
                in_=dec_bf[c0].rearrange("p c j -> p (c j)"),
            )

        def doc_operand(a, j0, j1):
            return doc_words(a, j0, j1).bitcast(FP8X4), doc_s[j0 // 512][:, a, :].bitcast(U8)[:, j0 % 512 : j0 % 512 + j1 - j0]

        def encode_pass(acc, ts, a, j0, j1, closes=True, first=0, last=LAST):
            width = j1 - j0
            rhs, rhs_scale = doc_operand(a, j0, j1)
            for u, t in enumerate(ts):
                nc.tensor.matmul_mx(
                    out=acc[:, u * width : (u + 1) * width],
                    lhsT=enc_w[a][:, t * P : (t + 1) * P].bitcast(FP8X4),
                    lhsT_scale=enc_s[a][:, t * P : (t + 1) * P],
                    rhs=rhs,
                    rhs_scale=rhs_scale,
                    start=(a == first and u == 0),
                    stop=(closes and a == last and u == len(ts) - 1),
                )

        def add_bias(acc, j0):
            code_bf[j0] = kept([P, P, 4], BF16, "code_bf%d" % j0)
            nc.vector.tensor_tensor(
                code_bf[j0][:].rearrange("p (c i) t -> p c t i", i=2),
                acc[:].rearrange("p (t c i) -> p c t i", t=4, i=2),
                bias[:].unsqueeze(1).unsqueeze(3).to_broadcast([P, P // 2, 4, 2]),
                ALU.add,
            )

        def clip(j0):
            flat = code_bf[j0][:].rearrange("p c t -> p (c t)")
            nc.vector.tensor_scalar(flat, flat, 0.0, None, ALU.max)

        def relu(acc, ts, j0, width=STRETCH):
            if j0 not in planes:
                planes[j0] = kept([P, 4, width], BF16, "planes%d" % j0)
            for u, t in enumerate(ts):
                nc.scalar.activation(
                    planes[j0][:, t, :], acc[:, u * width : (u + 1) * width], ACT.Relu, bias=bias[:, t : t + 1]
                )

        def interleave(j0, engine_copy=nc.scalar.copy, width=STRETCH):
            if j0 not in code_bf:
                code_bf[j0] = kept([P, width, 4], BF16, "code_bf%d" % j0)
            engine_copy(
                code_bf[j0][:].rearrange("p (c i) t -> p c t i", i=4),
                planes[j0][:].rearrange("p t (c i) -> p c t i", i=4),
            )

        def quant_code(j0, j1):
            nc.vector.quantize_mx(
                out=code_w[:, j0:j1].bitcast(FP8X4),
                scales=code_s[:, j0:j1],
                in_=code_bf[j0][:].rearrange("p c t -> p (c t)"),
            )

        def sketch(acc, n, j0, j1, start, stop):
            todo = [(a, g0, g1) for a in range(PASSES) for g0, g1 in doc_runs(a, j0, j1)]
            for i, (a, g0, g1) in enumerate(todo):
                rhs, rhs_scale = doc_operand(a, g0, g1)
                nc.tensor.matmul_mx(
                    out=acc[:, g0 - j0 : g1 - j0],
                    lhsT=sk_w[n][:, a, :].bitcast(U8).bitcast(FP4X4),
                    lhsT_scale=sk_s[n][:, a, :].bitcast(U8),
                    rhs=rhs,
                    rhs_scale=rhs_scale,
                    start=(start and i == 0),
                    stop=(stop and i == len(todo) - 1),
                )

        def doc_runs(a, j0, j1):
            cuts = [g for g in range(j0, j1, P) if g == j0 or doc_w[a, g][1] == g] + [j1]
            return list(zip(cuts[:-1], cuts[1:]))

        def decode(acc, n, j0, j1, start, stop):
            nc.tensor.matmul_mx(
                out=acc[:, 0 : j1 - j0],
                lhsT=dec_w[:, n * P : (n + 1) * P].bitcast(FP8X4),
                lhsT_scale=dec_s[:, n * P : (n + 1) * P],
                rhs=code_w[:, j0:j1].bitcast(FP8X4),
                rhs_scale=code_s[:, j0:j1],
                start=start,
                stop=stop,
            )

        def residual(acc, n, j0, j1, dst, sketch_first=True, opens=True):
            if sketch_first:
                sketch(acc, n, j0, j1, opens, False)
                decode(acc, n, j0, j1, False, True)
            else:
                decode(acc, n, j0, j1, opens, False)
                sketch(acc, n, j0, j1, False, True)
            nc.scalar.activation(dst, acc[:, 0 : j1 - j0], ACT.Abs)

        def sized(n, j0, j1, tag=None):
            size[n, j0] = kept([P, j1 - j0], F32, "size%d_%d" % (n, j0), tag)
            return size[n, j0][:]

        def scatter(n, j0, j1):
            window = cache[n % 3]
            nc.vector.tensor_tensor(
                window[:].indirect(place[:, j0 // 16 : j1 // 16]), size[n, j0][:], weight[:, j0:j1], ALU.mult
            )
            if j1 == S:
                nc.sync.dma_start(out[n * P : (n + 1) * P, :], window[:])

        tab_s = staged([P, T // 4], I32, "tab_s", 6 * SLOT - 1024)
        nc.gpsimd.memset(tab_s[:], 0)
        tab_w[0] = staged([P, T], I32, "tab_w0", SLOT // 2)
        load_table_columns(0, 0, T // 2)
        nc.sync.dma_start(pick[:], offs)
        for a in range(PASSES):
            row0 = SCALE_ROW0 + 4 * a
            nc.sync.dma_start(tab_s[row0 : row0 + 46 : 3, :], tab_scales[a].bitcast(I32))
        nc.scalar.dma_start(bias[:], benc.rearrange("(p t) -> p t", t=4))
        for rows in doc_s:
            nc.vector.memset(rows[:], 0)
        cache[0] = kept([P, T2], F32, "cache0")
        nc.vector.memset(cache[0][:].bitcast(I32), 0)
        load_table_columns(0, T // 2, T)
        load_enc(0, 2 * SLOT)
        load_table(1, 3 * SLOT)
        load_enc(1, 4 * SLOT)

        for j0 in (0, 512):
            nc.vector.tensor_copy(
                doc_s_rows[:, j0 : j0 + 512], tab_s[:].bitcast(U8).indirect(pick[:, j0 // 16 : j0 // 16 + 32])
            )
        cache[1] = staged([P, T2], F32, "cache1", 5 * SLOT)
        nc.gpsimd.memset(cache[1][:], 0.0)
        cast_enc(nc.scalar.copy, 0, 0, P)
        move_doc_scales(0)
        nc.sync.dma_start(place[:], offs2)
        load_enc(LAST, 6 * SLOT)
        for a in range(LAST):
            doc_tile(a, 0, S)
        gather_words(0, 0, S)
        load_table(LAST, SLOT)
        load_dec(0, 256)
        load_sketch_scales(0, EARLY)
        load_sketch(0, EARLY)
        move_doc_scales(1, 0, 3)
        load_weight(0, 256)
        move_doc_scales(1, 3, 4)
        load_weight(256, S)
        load_dec(256, 512)
        load_sketch(EARLY, ROW_TILES)
        load_sketch_scales(EARLY, ROW_TILES)
        load_dec(512, N)
        gather_words(1, 0, 512)
        quant_enc(0)
        gather_words(1, 512, S)
        cast_enc(nc.scalar.copy, 1, 0, 64)
        cast_enc(nc.vector.tensor_copy, 1, 64, P)
        quant_enc(1)
        cast_enc(nc.scalar.copy, LAST, 0, 40)
        cast_enc(nc.vector.tensor_copy, LAST, 40, P)
        quant_enc(LAST)

        halves = [(bank(0), (0, 1, 2, 3), 0, 128), (bank(1), (0, 1, 2, 3), 128, 256)]
        second = [(bank(2), (0, 1), 256, 512), (bank(6), (2,), 256, 512)]
        shared = bank(3)
        for a in range(LAST):
            for acc, ts, j0, j1 in halves + second:
                encode_pass(acc, ts, a, j0, j1)
            encode_pass(shared, (3,), a, 256, 512)

        doc_tile(LAST, 0, 256)
        doc_tile(LAST, 256, 512)
        gather_words(LAST, 0, 128)
        gather_words(LAST, 128, 256)
        gather_words(LAST, 256, 512)
        for acc, ts, j0, j1 in halves + second:
            encode_pass(acc, ts, LAST, j0, j1)
        encode_pass(shared, (3,), LAST, 256, 512, False)
        dec_bf[0] = staged([P, P, 4], BF16, "dec_bf0", 0)[:]
        code_bf[0] = staged([P, P, 4], BF16, "code_bf0", 1024)
        dec_bf[P] = kept([P, P, 4], BF16, "dec_bf128")[:]
        cast_dec_gpsimd(0, P)
        relu(halves[0][0], (0, 1, 2, 3), 0, P)
        add_bias(halves[1][0], P)
        interleave(0, nc.vector.tensor_copy, P)
        clip(P)
        quant_dec(0, P)
        for acc, ts, j0, j1 in halves:
            quant_code(j0, j1)
        cast_dec(P, 256)
        quant_dec(P, 256)
        for acc, ts, j0, j1 in second:
            relu(acc, ts, j0)
        doc_tile(LAST, 512, S, 0)
        gather_words(LAST, 512, S)
        first = sized(0, 0, 256)
        residual(bank(7), 0, 0, P, first[:, 0:P])
        residual(shared[:, STRETCH:], 0, P, 256, first[:, P:256], True, False)
        relu(shared, (3,), 256)
        scatter(0, 0, 256)
        interleave(256)
        quant_code(256, 512)
        residual(bank(4), 1, 0, 256, sized(1, 0, 256, "planes256"))
        scatter(1, 0, 256)

        def encode(banks, j0):
            for u, b in enumerate(banks):
                acc, ts = bank(b), (2 * u, 2 * u + 1)
                for a in (LAST, 0, 1):
                    encode_pass(acc, ts, a, j0, j0 + STRETCH, True, LAST, 1)
                relu(acc, ts, j0)

        encode((0, 3), 512)
        residual(bank(7), 0, 256, 512, sized(0, 256, 512))
        scatter(0, 256, 512)
        interleave(512)
        quant_code(512, 768)
        cache[2] = kept([P, T2], F32, "cache2", "code_bf512")
        nc.gpsimd.memset(cache[2][:], 0.0)
        residual(bank(4), 1, 256, 512, sized(1, 256, 512, "planes512"))
        scatter(1, 256, 512)

        planes[768] = staged([P, 4, STRETCH], BF16, "planes768", 7 * SLOT)
        encode((0, 7), 768)
        residual(bank(4), 0, 512, 768, sized(0, 512, 768))
        scatter(0, 512, 768)
        interleave(768)
        quant_code(768, S)
        size[1, 512] = staged([P, STRETCH], F32, "size1_512", 7 * SLOT)
        residual(bank(3), 1, 512, 768, size[1, 512][:])
        scatter(1, 512, 768)

        rest = staged([P, 512, 4], BF16, "dec_bf_rest", 7 * SLOT + 1024)
        dec_bf[256], dec_bf[512] = rest[:, 0:256, :], rest[:, 256:512, :]
        cast_dec(256, 512)
        quant_dec(256, 512)
        for n in range(EARLY):
            residual(bank((0, 7)[n]), n, 768, S, sized(n, 768, S))
            scatter(n, 768, S)
        cast_dec(512, N)
        quant_dec(512, N)
        for n, banks in zip(range(EARLY, ROW_TILES), ((4, 3), (0, 7), (2, 1), (6, 5))):
            whole = sized(n, 0, S)
            for half in range(2):
                j0 = 512 * half
                residual(bank(banks[half]), n, j0, j0 + 512, whole[:, j0 : j0 + 512], n < 4)
            scatter(n, 0, S)
